import numpy as np
import ml_dtypes


def mxq(x, axis, fmt="e4m3"):
    dtype, down = {"e4m3": (ml_dtypes.float8_e4m3fn, 7), "e5m2": (ml_dtypes.float8_e5m2, 14)}[fmt]
    v = np.moveaxis(np.asarray(x, np.float32).astype(ml_dtypes.bfloat16).astype(np.float64), axis, -1)
    blocks = v.reshape(v.shape[:-1] + (-1, 32))
    amax = np.abs(blocks).max(-1, keepdims=True)
    byte = np.maximum(np.where(amax > 0, np.frexp(amax)[1] - 1 + 127, 0) - down, 1)
    scale = np.exp2(byte - 127.0)
    codes = (blocks / scale).astype(np.float32).astype(dtype).astype(np.float64)
    return np.moveaxis((codes * scale).reshape(v.shape), -1, axis)


WIDE = False


def mx_kscale(k):
    if not WIDE:
        return np.ones(k)
    levels = np.array([10, -10, 5, -5, 0])
    if k % 512:
        return np.exp2(np.random.permutation(np.resize(levels, k // 32))).repeat(32)
    a = np.empty((k // 512, 16))
    for p in range(k // 512):
        a[p, :8] = np.random.permutation(np.resize(levels, 8))
        for g in range(8):
            far = levels[np.abs(levels - a[p, g]) >= 10]
            a[p, g + 8] = far[np.random.randint(len(far))]
    return np.exp2(a.ravel()).repeat(32)


BF16 = ml_dtypes.bfloat16


def bf(x):
    return np.asarray(x, np.float32).astype(BF16)


def f64(x):
    return np.asarray(x).astype(np.float64)


E2M1 = np.array([0.0, 0.5, 1.0, 1.5, 2.0, 3.0, 4.0, 6.0, -0.0, -0.5, -1.0, -1.5, -2.0, -3.0, -4.0, -6.0])


def pack_weight(w, fmt):
    k, n = w.shape
    w = f64(bf(w)).reshape(k // 32, 32, n)
    amax = np.abs(w).max(1)
    if fmt == "e4m3":
        byte = np.frexp(amax)[1] - 1 + 127 - 7
    else:
        mant, ex = np.frexp(amax / 6.0)
        byte = np.where(mant > 0.5, ex, ex - 1) + 127
    byte = np.clip(np.where(amax > 0, byte, 1), 1, 254)
    scaled = (w * np.exp2(127.0 - byte)[:, None, :]).reshape(k, n).astype(np.float32)
    by_word = np.ascontiguousarray(scaled.reshape(k // 512, 128, 4, n).transpose(0, 1, 3, 2))
    if fmt == "e4m3":
        words = by_word.astype(ml_dtypes.float8_e4m3fn).view(np.uint8)
    else:
        c = by_word.astype(ml_dtypes.float4_e2m1fn).view(np.uint8) & 0xF
        words = c[..., 0::2] | (c[..., 1::2] << 4)
    return np.ascontiguousarray(words), np.ascontiguousarray(byte.astype(np.uint8).reshape(k // 512, 16, n))


def unpack_weight(words, scales, fmt):
    g, p, n, _ = words.shape
    if fmt == "e4m3":
        vals = np.ascontiguousarray(words).view(ml_dtypes.float8_e4m3fn).astype(np.float64)
    else:
        nib = np.empty((g, p, n, 4), np.uint8)
        nib[..., 0::2] = words & 0xF
        nib[..., 1::2] = words >> 4
        vals = E2M1[nib]
    vals = vals * np.repeat(np.exp2(scales.astype(np.float64) - 127.0), 8, axis=1)[..., None]
    return vals.transpose(0, 1, 3, 2).reshape(g * 512, n)
def pack4(w):
    words, scales = pack_weight(w, "e2m1")
    return words.reshape(words.shape[0], 128, -1), scales


def unpack4(words, scales):
    return unpack_weight(words.reshape(words.shape[0], 128, -1, 2), scales, "e2m1")


def planes(Y):
    n, m = Y.shape
    b = f64(bf(Y)).reshape(n // 32, 32, m)
    amax = np.abs(b).max(1)
    byte = np.clip(np.where(amax > 0, np.frexp(amax)[1] - 1 + 127 - 7, 1), 1, 254)
    codes = (b * np.exp2(127.0 - byte)[:, None, :]).reshape(n, m).astype(np.float32).astype(ml_dtypes.float8_e4m3fn).view(np.uint8)
    words = codes.reshape(n // 512, 128, 4, m).transpose(0, 1, 3, 2)
    return np.ascontiguousarray(words), np.ascontiguousarray(byte.astype(np.uint8).reshape(n // 512, 16, m))


T, D, F = 1024, 1024, 1536

C = 1.702

def setup_inputs():
    s = mx_kscale(D)[:, None]
    x_words, x_scales = pack_weight(np.random.standard_normal((D, T)) * s, "e4m3")
    w_gate = bf(np.random.standard_normal((D, F)) / np.sqrt(D) / s)
    up_words, up_scales = pack_weight(np.random.standard_normal((D, F)) / np.sqrt(D) / s, "e4m3")
    down_words, down_scales = pack4(np.random.standard_normal((D, F)) / np.sqrt(D) / s)
    rate = bf(np.exp(0.8 * np.random.standard_normal((T, 1))))
    return {"x_words": x_words, "x_scales": x_scales, "w_gate": w_gate,
            "up_words": up_words, "up_scales": up_scales,
            "down_words": down_words, "down_scales": down_scales, "rate": rate}

def reference(x_words, x_scales, w_gate, up_words, up_scales, down_words, down_scales, rate):
    x = unpack_weight(x_words, x_scales, "e4m3").T
    wg = mxq(f64(w_gate), 0, "e4m3")
    wu = unpack_weight(up_words, up_scales, "e4m3")
    wd = unpack4(down_words, down_scales)
    a = x @ wg
    u = x @ wu
    d = x @ wd
    r = 1.0 / (1.0 + np.exp(-C * a))
    slope = r * (1.0 + C * a * (1.0 - r))
    y = slope * u * d * f64(rate)
    Y = y.reshape(T, F)
    words, scales = planes(Y)
    return y, words, scales

@@ -1,0 +1,293 @@
+from contextlib import ExitStack
+
+import concourse.mybir as mybir
+
+T, D, F = 1024, 1024, 1536
+C = 1.702
+FLOPS = 3 * 2 * T * D * F
+
+F32 = mybir.dt.float32
+BF16 = mybir.dt.bfloat16
+I32 = mybir.dt.int32
+U8 = mybir.dt.uint8
+FP8X4 = mybir.dt.float8_e4m3fn_x4
+FP4X4 = mybir.dt.float4_e2m1fn_x4
+ALU = mybir.AluOpType
+ACT = mybir.ActivationFunctionType
+
+P = 128
+PACK = 4
+SPAN = P * PACK
+PASSES = D // SPAN
+TOKEN_GROUPS = T // SPAN
+N = 512
+HALF = N // 2
+CHUNKS = F // N
+GROUPS = CHUNKS * TOKEN_GROUPS
+UNITS = GROUPS * PACK
+HEAD_SPLIT = 320
+
+
+def tile_geglu_recompute_gate_descent_k3_kernel(
+    tc, x_words, x_scales, w_gate, up_words, up_scales, down_words, down_scales, rate, out_0, out_1, out_2
+):
+    nc = tc.nc
+    with ExitStack() as ctx:
+        keep = ctx.enter_context(tc.tile_pool(name="keep", bufs=1))
+        work = ctx.enter_context(tc.tile_pool(name="work", bufs=3))
+        psum = ctx.enter_context(tc.psum_pool(name="psum", bufs=2))
+        ctx.enter_context(tc.manual_schedule())
+
+        x_raw = keep.tile([P, TOKEN_GROUPS, PASSES, SPAN], I32, align_bytes=64)
+        x_codes = keep.tile([P, TOKEN_GROUPS, PASSES, PACK, P], I32, align_bytes=64)
+        xs_raw = keep.tile([P, PASSES, T], U8, align_bytes=64)
+        x_plane = keep.tile([P, TOKEN_GROUPS, PASSES, PACK, P], U8, align_bytes=64)
+        gate_raw = keep.tile([P, CHUNKS, PASSES, PACK, N], BF16, align_bytes=64)
+        gate_grouped = keep.tile([P, CHUNKS, PASSES, N, PACK], BF16, align_bytes=64)
+        gate_codes = keep.tile([P, CHUNKS, PASSES, N], I32, align_bytes=64)
+        gate_plane = keep.tile([P, CHUNKS, PASSES, N], U8, align_bytes=64)
+        up_codes = keep.tile([P, CHUNKS, PASSES, N], I32, align_bytes=64)
+        up_plane = keep.tile([P, PASSES, F], U8, align_bytes=64)
+        down_codes = keep.tile([P, CHUNKS, PASSES, 2 * N], U8, align_bytes=64)
+        down_plane = keep.tile([P, PASSES, F], U8, align_bytes=64)
+        rate_raw = keep.tile([P, TOKEN_GROUPS, PACK], BF16)
+        factor = keep.tile([P, TOKEN_GROUPS, PACK], F32)
+        zero_in = keep.tile([P, 1], F32)
+        zero_bias = keep.tile([P, 1], F32)
+        y = keep.tile([P, GROUPS, PACK, N], F32, align_bytes=64)
+        y_grouped = keep.tile([P, GROUPS, N, PACK], BF16, align_bytes=64)
+        y_codes = keep.tile([P, GROUPS, N], I32, align_bytes=64)
+        y_plane = keep.tile([P, CHUNKS, TOKEN_GROUPS, N], U8, align_bytes=64)
+
+        x_src = x_words.rearrange("g p n t -> p g (n t)").bitcast(I32)
+        up_src = up_words.rearrange("g p n t -> p g (n t)").bitcast(I32)
+        down_src = down_words.rearrange("g p b -> p g b").bitcast(I32)
+        codes_dst = out_1.rearrange("g p n t -> p g (n t)").bitcast(I32)
+        y_dst = out_0.rearrange("(g p t) n -> p g t n", p=P, t=PACK)
+
+        def load_scale_rows(plane, scales):
+            for q in range(4):
+                nc.sync.dma_start(
+                    out=plane[:].bitcast(I32)[32 * q : 32 * q + 4],
+                    in_=scales.bitcast(I32)[:, 4 * q : 4 * q + 4, :].rearrange("g r n -> r g n"),
+                )
+
+        def load_x(tg):
+            nc.sync.dma_start(out=x_raw[:, tg], in_=x_src[:, :, SPAN * tg : SPAN * (tg + 1)])
+
+        def load_gate(c, g):
+            rows = w_gate[SPAN * g : SPAN * (g + 1), N * c : N * (c + 1)]
+            nc.sync.dma_start(out=gate_raw[:, c, g], in_=rows.rearrange("(p j) n -> p j n", j=PACK))
+
+        def load_up_down(c):
+            nc.sync.dma_start(out=up_codes[:, c], in_=up_src[:, :, N * c : N * (c + 1)])
+            nc.sync.dma_start(
+                out=down_codes[:, c].bitcast(I32),
+                in_=down_src[:, :, HALF * c : HALF * (c + 1)],
+            )
+
+        def permute_x_codes(tg):
+            nc.vector.tensor_copy(
+                out=x_codes[:, tg].rearrange("p g t m -> p g m t"),
+                in_=x_raw[:, tg].rearrange("p g (m t) -> p g m t", t=PACK),
+            )
+
+        def permute_x_scales(tg):
+            nc.vector.tensor_copy(
+                out=x_plane[:, tg],
+                in_=xs_raw[:, :, SPAN * tg : SPAN * (tg + 1)].rearrange("p g (m t) -> p g t m", t=PACK),
+            )
+
+        def interleave(on_vector, dst, src, run):
+            out = dst.rearrange("p (c i) t -> p c t i", i=run)
+            in_ = src.rearrange("p t (c i) -> p c t i", i=run)
+            if on_vector:
+                nc.vector.tensor_copy(out=out, in_=in_)
+            else:
+                nc.scalar.copy(out=out, in_=in_)
+
+        def group_gate(on_vector, c, g, lo, hi):
+            interleave(on_vector, gate_grouped[:, c, g, lo:hi, :], gate_raw[:, c, g, :, lo:hi], 4)
+
+        def quantize_gate(c, g):
+            nc.vector.quantize_mx(
+                out=gate_codes[:, c, g].bitcast(FP8X4),
+                scales=gate_plane[:, c, g],
+                in_=gate_grouped[:, c, g].rearrange("p n t -> p (n t)"),
+            )
+
+        def group_y(on_vector, j, lo, hi):
+            interleave(on_vector, y_grouped[:, j, lo:hi, :], y[:, j, :, lo:hi], 2)
+
+        def quantize_y(j, lo, hi):
+            c, tg = divmod(j, TOKEN_GROUPS)
+            nc.vector.quantize_mx(
+                out=y_codes[:, j, lo:hi].bitcast(FP8X4),
+                scales=y_plane[:, c, tg, lo:hi],
+                in_=y_grouped[:, j, lo:hi, :].rearrange("p n t -> p (n t)"),
+            )
+            nc.sync.dma_start(out=codes_dst[:, tg, N * c + lo : N * c + hi], in_=y_codes[:, j, lo:hi])
+
+        def store_y_scales(c):
+            for q in range(4):
+                nc.sync.dma_start(
+                    out=out_2.bitcast(I32)[:, 4 * q : 4 * q + 4, P * c : P * (c + 1)].rearrange("g r n -> r g n"),
+                    in_=y_plane[:].bitcast(I32)[32 * q : 32 * q + 4, c],
+                )
+
+        def product(acc, i, codes, plane):
+            tg, t = (i // PACK) % TOKEN_GROUPS, i % PACK
+            for g in range(PASSES):
+                nc.tensor.matmul_mx(
+                    out=acc[:],
+                    lhsT=x_codes[:, tg, g, t].bitcast(FP8X4),
+                    lhsT_scale=x_plane[:, tg, g, t],
+                    rhs=codes[g],
+                    rhs_scale=plane[g],
+                    start=(g == 0),
+                    stop=(g == PASSES - 1),
+                )
+
+        banks = {}
+        parts = {}
+
+        def gate_product(i):
+            c = i // (PACK * TOKEN_GROUPS)
+            acc = psum.tile([P, N], F32, name="a", tag="a", bufs=2)
+            product(
+                acc,
+                i,
+                [gate_codes[:, c, g].bitcast(FP8X4) for g in range(PASSES)],
+                [gate_plane[:, c, g] for g in range(PASSES)],
+            )
+            banks["a", i] = acc
+
+        def up_down_products(i):
+            c = i // (PACK * TOKEN_GROUPS)
+            u = psum.tile([P, N], F32, name="u", tag="u", bufs=3)
+            product(
+                u,
+                i,
+                [up_codes[:, c, g].bitcast(FP8X4) for g in range(PASSES)],
+                [up_plane[:, g, N * c : N * (c + 1)] for g in range(PASSES)],
+            )
+            d = psum.tile([P, N], F32, name="d", tag="d", bufs=3)
+            product(
+                d,
+                i,
+                [down_codes[:, c, g].bitcast(FP4X4) for g in range(PASSES)],
+                [down_plane[:, g, N * c : N * (c + 1)] for g in range(PASSES)],
+            )
+            banks["u", i] = u
+            banks["d", i] = d
+
+        def activations(i):
+            a = banks["a", i]
+            th = work.tile([P, N], F32, name="th", tag="th", bufs=3)
+            nc.scalar.activation(out=th[:], in_=a[:], func=ACT.Tanh, bias=zero_bias[:], scale=C / 2)
+            sn = work.tile([P, N], F32, name="sn", tag="sn", bufs=3)
+            nc.scalar.activation(out=sn[:], in_=a[:], func=ACT.Silu, bias=zero_bias[:], scale=-C)
+            parts["th", i] = th
+            parts["sn", i] = sn
+
+        def drain_products(i):
+            left = work.tile([P, N], F32, name="left", tag="left", bufs=3)
+            nc.vector.scalar_tensor_tensor(
+                out=left[:], in0=parts["th", i][:], scalar=1.0, in1=banks["u", i][:], op0=ALU.add, op1=ALU.mult
+            )
+            right = work.tile([P, N], F32, name="right", tag="right", bufs=3)
+            nc.vector.scalar_tensor_tensor(
+                out=right[:], in0=parts["sn", i][:], scalar=1.0, in1=banks["d", i][:], op0=ALU.subtract, op1=ALU.mult
+            )
+            parts["left", i] = left
+            parts["right", i] = right
+
+        def finish(i, lo, hi):
+            j, t = divmod(i, PACK)
+            c, tg = divmod(j, TOKEN_GROUPS)
+            nc.vector.scalar_tensor_tensor(
+                out=y[:, j, t, lo:hi],
+                in0=parts["left", i][:, lo:hi],
+                scalar=factor[:, tg, t : t + 1],
+                in1=parts["right", i][:, lo:hi],
+                op0=ALU.mult,
+                op1=ALU.mult,
+            )
+            nc.sync.dma_start(out=y_dst[:, tg, t, N * c + lo : N * c + hi], in_=y[:, j, t, lo:hi])
+
+        nc.vector.memset(xs_raw[:].bitcast(I32), 0)
+        nc.vector.memset(zero_in[:], 0.0)
+        nc.vector.memset(up_plane[:].bitcast(I32), 0)
+        nc.vector.memset(down_plane[:].bitcast(I32), 0)
+        nc.scalar.activation(out=zero_bias[:], in_=zero_in[:], func=ACT.Silu)
+        nc.gpsimd.dma_start(out=rate_raw[:], in_=rate.rearrange("(g p t) o -> p g (t o)", p=P, t=PACK))
+        nc.gpsimd.tensor_scalar(
+            out=factor[:], in0=rate_raw[:], scalar1=-0.5, scalar2=0.0, op0=ALU.mult, op1=ALU.add
+        )
+
+        load_x(0)
+        load_scale_rows(xs_raw, x_scales)
+        load_gate(0, 0)
+        load_gate(0, 1)
+        load_up_down(0)
+        load_scale_rows(up_plane, up_scales)
+        load_scale_rows(down_plane, down_scales)
+        load_x(1)
+        for c in range(1, CHUNKS):
+            load_gate(c, 0)
+            load_gate(c, 1)
+            load_up_down(c)
+
+        permute_x_codes(0)
+        permute_x_scales(0)
+        group_gate(True, 0, 0, 0, HEAD_SPLIT)
+        group_gate(False, 0, 0, HEAD_SPLIT, N)
+        group_gate(False, 0, 1, HEAD_SPLIT, N)
+        group_gate(True, 0, 1, 0, HEAD_SPLIT)
+        quantize_gate(0, 0)
+        quantize_gate(0, 1)
+        permute_x_scales(1)
+        permute_x_codes(1)
+
+        scalar_extra = {
+            1: ("gate", 1, 0, 0), 2: ("gate", 1, 0, 1), 3: ("gate", 1, 1, 0), 4: ("gate", 1, 1, 1),
+            6: ("y", 0, 0), 7: ("y", 0, 1), 8: ("gate", 2, 0, 0), 9: ("gate", 2, 0, 1),
+            11: ("gate", 2, 1, 0), 12: ("gate", 2, 1, 1), 13: ("y", 1, 0), 14: ("y", 1, 1),
+            15: ("y", 2, 0), 17: ("y", 2, 1), 18: ("y", 3, 0), 19: ("y", 3, 1),
+            21: ("y", 4, 0), 22: ("y", 4, 1),
+        }
+        vector_extra = {
+            3: ("gate", 1, 0), 5: ("gate", 1, 1), 8: ("y", 0), 10: ("gate", 2, 0), 13: ("gate", 2, 1),
+            15: ("y", 1), 18: ("y", 2), 20: ("y", 3), 23: ("y", 4),
+        }
+
+        gate_product(0)
+        for i in range(UNITS):
+            if i + 1 < UNITS:
+                gate_product(i + 1)
+            up_down_products(i)
+            activations(i)
+            extra = scalar_extra.get(i)
+            if extra is not None and extra[0] == "gate":
+                group_gate(False, extra[1], extra[2], HALF * extra[3], HALF * (extra[3] + 1))
+            if extra is not None and extra[0] == "y":
+                group_y(False, extra[1], HALF * extra[2], HALF * (extra[2] + 1))
+            drain_products(i)
+            if i > 0:
+                finish(i - 1, 0, N)
+            extra = vector_extra.get(i)
+            if extra is not None and extra[0] == "gate":
+                quantize_gate(extra[1], extra[2])
+            if extra is not None and extra[0] == "y":
+                quantize_y(extra[1], 0, N)
+                if extra[1] % TOKEN_GROUPS == TOKEN_GROUPS - 1:
+                    store_y_scales(extra[1] // TOKEN_GROUPS)
+
+        last = UNITS - 1
+        finish(last, 0, HALF)
+        finish(last, HALF, N)
+        group_y(False, GROUPS - 1, 0, HALF)
+        group_y(True, GROUPS - 1, HALF, N)
+        quantize_y(GROUPS - 1, 0, HALF)
+        quantize_y(GROUPS - 1, HALF, N)
+        store_y_scales(CHUNKS - 1)

@@ -20,12 +20,48 @@ PACK = 4
 SPAN = P * PACK
 PASSES = D // SPAN
 TOKEN_GROUPS = T // SPAN
-N = 512
-HALF = N // 2
-CHUNKS = F // N
+BANK = 512
+UP_ROW = 4
+BUFS = {"sn": 5, "th": 4, "left": 4, "right": 5, "rated": 1}
+WIDTHS = [256, 512, 512, 256]
+STARTS = [sum(WIDTHS[:c]) for c in range(len(WIDTHS))]
+CHUNKS = len(WIDTHS)
 GROUPS = CHUNKS * TOKEN_GROUPS
-UNITS = GROUPS * PACK
-HEAD_SPLIT = 320
+UNITS = [
+    (c, tg, t0)
+    for c in range(CHUNKS)
+    for tg in range(TOKEN_GROUPS)
+    for t0 in range(0, PACK, BANK // WIDTHS[c])
+]
+ORDER = [
+    ("Lg", 0, 1), ("Ls", "S", "x", 2), ("Lh", 1), ("Lg", 0, 0), ("Ls", "S", "x", 3), ("Lh", 0), ("Ls", "S", "x", 0), ("Ls", "S", "x", 1), ("Ls", "S", "up", 1), ("Lg", 1, 1), ("Ls", "S", "up", 2), ("Lx",), ("Ls", "S", "up", 3), ("Lu", 0), ("Ls", "S", "up", 0), ("Ls", "S", "down", 2), ("Lg", 1, 0), ("Ls", "S", "down", 3), ("Ls", "S", "down", 0), ("Ls", "S", "down", 1), ("Ld", 0), ("Lg", 2, 1), ("Lu", 1), ("Lg", 3, 0), ("Ld", 3), ("Ld", 1), ("Lg", 3, 1), ("Ld", 2), ("Lg", 2, 0), ("Lu", 3), ("Lu", 2), ("R",), ("G", "A", 0, 1, 0, 128), ("G", "V", 0, 1, 128, 256), ("PXH", 1), ("PXS", 0), ("PXH", 0), ("G", "A", 0, 0, 128, 256), ("G", "A", 0, 0, 0, 128), ("QG", 0, 1), ("G", "A", 1, 1, 0, 256), ("QG", 0, 0), ("PXS", 1), ("G", "V", 1, 1, 256, 512), ("PXC", 1), ("QG", 1, 1),
+    ("M", 0, 0), ("M", 1, 0), ("M", 1, 1), ("M", 0, 1), ("ACT", 0), ("ACT", 1), ("G", "A", 1, 0, 256, 512), ("A", 0), ("G", "V", 1, 0, 0, 256),
+    ("M", 2, 0), ("M", 2, 1), ("M", 1, 2), ("M", 0, 2), ("ACT", 2), ("A", 1), ("B", 1), ("Bp", 0), ("QG", 1, 0), ("C", 1), ("G", "V", 2, 1, 256, 512),
+    ("M", 3, 0), ("G", "A", 2, 1, 0, 256), ("ACT", 3), ("TS", 0), ("TT", 0), ("A", 2),
+    ("M", 3, 1), ("M", 2, 2), ("M", 3, 2), ("G", "A", 3, 0, 0, 256), ("A", 3), ("B", 3), ("Bp", 2), ("C", 3), ("Y", "V", 0, 0, 256),
+    ("M", 4, 1), ("M", 4, 0), ("M", 4, 2), ("ACT", 4), ("TS", 2), ("TT", 2), ("A", 4),
+    ("M", 5, 1), ("M", 5, 0), ("M", 5, 2), ("ACT", 5), ("G", "A", 2, 0, 0, 256), ("A", 5), ("B", 5), ("Bp", 4), ("C", 5), ("G", "V", 2, 0, 256, 512),
+    ("M", 6, 1), ("M", 6, 0), ("M", 6, 2), ("ACT", 6), ("TS", 4), ("TT", 4), ("A", 6),
+    ("M", 7, 1), ("M", 7, 0), ("M", 7, 2), ("ACT", 7), ("G", "A", 3, 1, 0, 256), ("A", 7), ("B", 7), ("Bp", 6), ("C", 7), ("QG", 2, 0),
+    ("M", 8, 1), ("M", 8, 0), ("M", 8, 2), ("ACT", 8), ("TS", 6), ("TT", 6), ("A", 8),
+    ("M", 9, 1), ("M", 9, 0), ("M", 9, 2), ("ACT", 9), ("Y", "A", 1, 0, 256), ("A", 9), ("B", 9), ("Bp", 8), ("QG", 2, 1), ("C", 9),
+    ("M", 10, 1), ("M", 10, 0), ("M", 10, 2), ("ACT", 10), ("TS", 8), ("TT", 8), ("A", 10),
+    ("M", 11, 1), ("M", 11, 0), ("M", 11, 2), ("ACT", 11), ("A", 11), ("B", 11), ("Bp", 10), ("QY", 0), ("C", 11), ("QG", 3, 1),
+    ("M", 12, 1), ("M", 12, 0), ("M", 12, 2), ("ACT", 12), ("TS", 10), ("TT", 10), ("A", 12),
+    ("M", 13, 1), ("M", 13, 0), ("M", 13, 2), ("ACT", 13), ("Y", "A", 2, 0, 256), ("A", 13), ("B", 13), ("Bp", 12), ("C", 13), ("QY", 1),
+    ("M", 14, 1), ("M", 14, 0), ("M", 14, 2), ("ACT", 14), ("TS", 12), ("TT", 12), ("A", 14),
+    ("M", 15, 1), ("M", 15, 0), ("M", 15, 2), ("ACT", 15), ("Y", "A", 2, 256, 512), ("A", 15), ("B", 15), ("Bp", 14), ("C", 15), ("Y", "V", 3, 256, 512),
+    ("M", 16, 1), ("M", 16, 0), ("M", 16, 2), ("ACT", 16), ("TS", 14), ("TT", 14), ("A", 16),
+    ("M", 17, 1), ("M", 17, 0), ("M", 17, 2), ("ACT", 17), ("Y", "A", 3, 0, 256), ("A", 17), ("B", 17), ("Bp", 16), ("QG", 3, 0), ("C", 17), ("QY", 2),
+    ("M", 18, 1), ("M", 18, 0), ("M", 18, 2), ("ACT", 18), ("TS", 16), ("TT", 16), ("A", 18),
+    ("M", 19, 1), ("M", 19, 0), ("M", 19, 2), ("ACT", 19), ("Y", "A", 4, 0, 256), ("A", 19), ("B", 19), ("Bp", 18), ("C", 19), ("QY", 3),
+    ("M", 20, 1), ("M", 20, 0), ("M", 20, 2), ("ACT", 20), ("TS", 18), ("TT", 18), ("A", 20),
+    ("M", 21, 1), ("M", 21, 0), ("M", 21, 2), ("ACT", 21), ("Y", "A", 4, 256, 512), ("A", 21), ("B", 21), ("Bp", 20), ("C", 21), ("QY", 4),
+    ("M", 22, 1), ("M", 22, 0), ("M", 22, 2), ("ACT", 22), ("TS", 20), ("A", 22), ("B", 22),
+    ("M", 23, 1), ("M", 23, 0), ("M", 23, 2), ("ACT", 23), ("Y", "A", 5, 0, 256), ("Y", "A", 5, 256, 512), ("TT", 20), ("A", 23), ("B", 23), ("C", 22), ("QY", 5), ("C", 23),
+    ("Y", "A", 6, 0, 256), ("Y", "A", 7, 128, 256), ("Y", "V", 7, 0, 128), ("QY", 6), ("QY", 7),
+
+]
 
 
 def tile_geglu_recompute_gate_descent_k3_kernel(
@@ -38,256 +74,333 @@ def tile_geglu_recompute_gate_descent_k3_kernel(
         psum = ctx.enter_context(tc.psum_pool(name="psum", bufs=2))
         ctx.enter_context(tc.manual_schedule())
 
-        x_raw = keep.tile([P, TOKEN_GROUPS, PASSES, SPAN], I32, align_bytes=64)
-        x_codes = keep.tile([P, TOKEN_GROUPS, PASSES, PACK, P], I32, align_bytes=64)
-        xs_raw = keep.tile([P, PASSES, T], U8, align_bytes=64)
-        x_plane = keep.tile([P, TOKEN_GROUPS, PASSES, PACK, P], U8, align_bytes=64)
-        gate_raw = keep.tile([P, CHUNKS, PASSES, PACK, N], BF16, align_bytes=64)
-        gate_grouped = keep.tile([P, CHUNKS, PASSES, N, PACK], BF16, align_bytes=64)
-        gate_codes = keep.tile([P, CHUNKS, PASSES, N], I32, align_bytes=64)
-        gate_plane = keep.tile([P, CHUNKS, PASSES, N], U8, align_bytes=64)
-        up_codes = keep.tile([P, CHUNKS, PASSES, N], I32, align_bytes=64)
-        up_plane = keep.tile([P, PASSES, F], U8, align_bytes=64)
-        down_codes = keep.tile([P, CHUNKS, PASSES, 2 * N], U8, align_bytes=64)
-        down_plane = keep.tile([P, PASSES, F], U8, align_bytes=64)
-        rate_raw = keep.tile([P, TOKEN_GROUPS, PACK], BF16)
-        factor = keep.tile([P, TOKEN_GROUPS, PACK], F32)
-        zero_in = keep.tile([P, 1], F32)
-        zero_bias = keep.tile([P, 1], F32)
-        y = keep.tile([P, GROUPS, PACK, N], F32, align_bytes=64)
-        y_grouped = keep.tile([P, GROUPS, N, PACK], BF16, align_bytes=64)
-        y_codes = keep.tile([P, GROUPS, N], I32, align_bytes=64)
-        y_plane = keep.tile([P, CHUNKS, TOKEN_GROUPS, N], U8, align_bytes=64)
+        def kept(name, shape, dtype):
+            return keep.tile(shape, dtype, name=name, align_bytes=64)
+
+        x_raw = [kept("x_raw%d" % tg, [P, PASSES, SPAN], I32) for tg in range(TOKEN_GROUPS)]
+        x_codes = [kept("x_codes%d" % tg, [P, PASSES, PACK, P], I32) for tg in range(TOKEN_GROUPS)]
+        xs_raw = kept("xs_raw", [P, PASSES, T], U8)
+        x_plane = [kept("x_plane%d" % tg, [P, PASSES, PACK, P], U8) for tg in range(TOKEN_GROUPS)]
+        gate_raw = [kept("gate_raw%d" % c, [P, PASSES, PACK, w], BF16) for c, w in enumerate(WIDTHS)]
+        gate_grouped = [kept("gate_grouped%d" % c, [P, PASSES, w, PACK], BF16) for c, w in enumerate(WIDTHS)]
+        gate_codes = [kept("gate_codes%d" % c, [P, PASSES, w], I32) for c, w in enumerate(WIDTHS)]
+        gate_plane = [kept("gate_plane%d" % c, [P, PASSES, w], U8) for c, w in enumerate(WIDTHS)]
+        up_codes = [kept("up_codes%d" % c, [P, PASSES, w], I32) for c, w in enumerate(WIDTHS)]
+        up_plane = kept("up_plane", [P, PASSES, F], U8)
+        down_codes = [kept("down_codes%d" % c, [P, PASSES, 2 * w], U8) for c, w in enumerate(WIDTHS)]
+        down_plane = kept("down_plane", [P, PASSES, F], U8)
+        rate_raw = kept("rate_raw", [P, TOKEN_GROUPS, PACK], BF16)
+        minus_half_rate = kept("minus_half_rate", [P, TOKEN_GROUPS, PACK], F32)
+        half_rate = kept("half_rate", [P, TOKEN_GROUPS, PACK], F32)
+        zero_in = kept("zero_in", [P, 1], F32)
+        zero_bias = kept("zero_bias", [P, 1], F32)
+        group_width = [WIDTHS[j // TOKEN_GROUPS] for j in range(GROUPS)]
+        y = [kept("y%d" % j, [P, PACK, w], F32) for j, w in enumerate(group_width)]
+        y_grouped = [kept("y_grouped%d" % j, [P, w, PACK], BF16) for j, w in enumerate(group_width)]
+        y_codes = [kept("y_codes%d" % j, [P, w], I32) for j, w in enumerate(group_width)]
+        y_plane = [kept("y_plane%d" % c, [P, TOKEN_GROUPS, w], U8) for c, w in enumerate(WIDTHS)]
 
         x_src = x_words.rearrange("g p n t -> p g (n t)").bitcast(I32)
         up_src = up_words.rearrange("g p n t -> p g (n t)").bitcast(I32)
         down_src = down_words.rearrange("g p b -> p g b").bitcast(I32)
         codes_dst = out_1.rearrange("g p n t -> p g (n t)").bitcast(I32)
         y_dst = out_0.rearrange("(g p t) n -> p g t n", p=P, t=PACK)
+        planes = {"x": (xs_raw, x_scales), "up": (up_plane, up_scales), "down": (down_plane, down_scales)}
+        engines = {"V": nc.vector, "G": nc.gpsimd, "S": nc.sync, "A": nc.scalar}
 
-        def load_scale_rows(plane, scales):
-            for q in range(4):
-                nc.sync.dma_start(
-                    out=plane[:].bitcast(I32)[32 * q : 32 * q + 4],
-                    in_=scales.bitcast(I32)[:, 4 * q : 4 * q + 4, :].rearrange("g r n -> r g n"),
+        def clear_plane(engine, name):
+            engines[engine].memset(planes[name][0][:].bitcast(I32), 0)
+
+        def load_scale_rows(engine, name, q):
+            plane, scales = planes[name]
+            row = 32 * q + (UP_ROW if name == "up" else 0)
+            engines[engine].dma_start(
+                out=plane[:].bitcast(I32)[row : row + 4],
+                in_=scales.bitcast(I32)[:, 4 * q : 4 * q + 4, :].rearrange("g r n -> r g n"),
+            )
+
+        def warm_table():
+            nc.vector.memset(zero_in[:], 0.0)
+            nc.scalar.activation(out=zero_bias[:], in_=zero_in[:], func=ACT.Silu)
+
+        def load_rate(engine):
+            engines[engine].dma_start(out=rate_raw[:], in_=rate.rearrange("(g p t) o -> p g (t o)", p=P, t=PACK))
+
+        def scale_rate():
+            for dst, by in ((minus_half_rate, -0.5), (half_rate, 0.5)):
+                nc.gpsimd.tensor_scalar(
+                    out=dst[:], in0=rate_raw[:], scalar1=by, scalar2=0.0, op0=ALU.mult, op1=ALU.add
                 )
 
         def load_x(tg):
-            nc.sync.dma_start(out=x_raw[:, tg], in_=x_src[:, :, SPAN * tg : SPAN * (tg + 1)])
+            nc.sync.dma_start(out=x_raw[tg][:], in_=x_src[:, :, SPAN * tg : SPAN * (tg + 1)])
+
+        def load_x_pass(g):
+            nc.sync.dma_start(out=x_raw[0][:, g], in_=x_src[:, g, 0:SPAN])
+
+        def permute_x_pass(g):
+            nc.vector.tensor_copy(
+                out=x_codes[0][:, g].rearrange("p t m -> p m t"),
+                in_=x_raw[0][:, g].rearrange("p (m t) -> p m t", t=PACK),
+            )
 
         def load_gate(c, g):
-            rows = w_gate[SPAN * g : SPAN * (g + 1), N * c : N * (c + 1)]
-            nc.sync.dma_start(out=gate_raw[:, c, g], in_=rows.rearrange("(p j) n -> p j n", j=PACK))
+            rows = w_gate[SPAN * g : SPAN * (g + 1), STARTS[c] : STARTS[c] + WIDTHS[c]]
+            nc.sync.dma_start(out=gate_raw[c][:, g], in_=rows.rearrange("(p j) n -> p j n", j=PACK))
 
-        def load_up_down(c):
-            nc.sync.dma_start(out=up_codes[:, c], in_=up_src[:, :, N * c : N * (c + 1)])
+        def load_up(c):
+            nc.sync.dma_start(out=up_codes[c][:], in_=up_src[:, :, STARTS[c] : STARTS[c] + WIDTHS[c]])
+
+        def load_down(c):
             nc.sync.dma_start(
-                out=down_codes[:, c].bitcast(I32),
-                in_=down_src[:, :, HALF * c : HALF * (c + 1)],
+                out=down_codes[c][:].bitcast(I32),
+                in_=down_src[:, :, STARTS[c] // 2 : (STARTS[c] + WIDTHS[c]) // 2],
             )
 
         def permute_x_codes(tg):
             nc.vector.tensor_copy(
-                out=x_codes[:, tg].rearrange("p g t m -> p g m t"),
-                in_=x_raw[:, tg].rearrange("p g (m t) -> p g m t", t=PACK),
+                out=x_codes[tg][:].rearrange("p g t m -> p g m t"),
+                in_=x_raw[tg][:].rearrange("p g (m t) -> p g m t", t=PACK),
             )
 
         def permute_x_scales(tg):
             nc.vector.tensor_copy(
-                out=x_plane[:, tg],
+                out=x_plane[tg][:],
                 in_=xs_raw[:, :, SPAN * tg : SPAN * (tg + 1)].rearrange("p g (m t) -> p g t m", t=PACK),
             )
 
-        def interleave(on_vector, dst, src, run):
+        def interleave(engine, dst, src, run):
             out = dst.rearrange("p (c i) t -> p c t i", i=run)
             in_ = src.rearrange("p t (c i) -> p c t i", i=run)
-            if on_vector:
+            if engine == "V":
                 nc.vector.tensor_copy(out=out, in_=in_)
+            elif engine == "G":
+                nc.gpsimd.tensor_scalar(
+                    out=dst, in0=src.rearrange("p t n -> p n t"), scalar1=1.0, scalar2=-0.0, op0=ALU.mult, op1=ALU.add
+                )
             else:
                 nc.scalar.copy(out=out, in_=in_)
 
-        def group_gate(on_vector, c, g, lo, hi):
-            interleave(on_vector, gate_grouped[:, c, g, lo:hi, :], gate_raw[:, c, g, :, lo:hi], 4)
+        def group_gate(engine, c, g, lo, hi):
+            interleave(engine, gate_grouped[c][:, g, lo:hi, :], gate_raw[c][:, g, :, lo:hi], 4)
 
         def quantize_gate(c, g):
             nc.vector.quantize_mx(
-                out=gate_codes[:, c, g].bitcast(FP8X4),
-                scales=gate_plane[:, c, g],
-                in_=gate_grouped[:, c, g].rearrange("p n t -> p (n t)"),
+                out=gate_codes[c][:, g].bitcast(FP8X4),
+                scales=gate_plane[c][:, g],
+                in_=gate_grouped[c][:, g].rearrange("p n t -> p (n t)"),
             )
 
-        def group_y(on_vector, j, lo, hi):
-            interleave(on_vector, y_grouped[:, j, lo:hi, :], y[:, j, :, lo:hi], 2)
+        def group_y(engine, j, lo, hi):
+            interleave(engine, y_grouped[j][:, lo:hi, :], y[j][:, :, lo:hi], 2)
 
-        def quantize_y(j, lo, hi):
+        def quantize_y(j):
             c, tg = divmod(j, TOKEN_GROUPS)
             nc.vector.quantize_mx(
-                out=y_codes[:, j, lo:hi].bitcast(FP8X4),
-                scales=y_plane[:, c, tg, lo:hi],
-                in_=y_grouped[:, j, lo:hi, :].rearrange("p n t -> p (n t)"),
+                out=y_codes[j][:].bitcast(FP8X4),
+                scales=y_plane[c][:, tg],
+                in_=y_grouped[j][:].rearrange("p n t -> p (n t)"),
             )
-            nc.sync.dma_start(out=codes_dst[:, tg, N * c + lo : N * c + hi], in_=y_codes[:, j, lo:hi])
+
+        def store_y_codes(j):
+            c, tg = divmod(j, TOKEN_GROUPS)
+            nc.sync.dma_start(out=codes_dst[:, tg, STARTS[c] : STARTS[c] + WIDTHS[c]], in_=y_codes[j][:])
 
         def store_y_scales(c):
+            cols = slice(STARTS[c] // 4, (STARTS[c] + WIDTHS[c]) // 4)
             for q in range(4):
                 nc.sync.dma_start(
-                    out=out_2.bitcast(I32)[:, 4 * q : 4 * q + 4, P * c : P * (c + 1)].rearrange("g r n -> r g n"),
-                    in_=y_plane[:].bitcast(I32)[32 * q : 32 * q + 4, c],
-                )
-
-        def product(acc, i, codes, plane):
-            tg, t = (i // PACK) % TOKEN_GROUPS, i % PACK
-            for g in range(PASSES):
-                nc.tensor.matmul_mx(
-                    out=acc[:],
-                    lhsT=x_codes[:, tg, g, t].bitcast(FP8X4),
-                    lhsT_scale=x_plane[:, tg, g, t],
-                    rhs=codes[g],
-                    rhs_scale=plane[g],
-                    start=(g == 0),
-                    stop=(g == PASSES - 1),
+                    out=out_2.bitcast(I32)[:, 4 * q : 4 * q + 4, cols].rearrange("g r n -> r g n"),
+                    in_=y_plane[c][:].bitcast(I32)[32 * q : 32 * q + 4],
                 )
 
         banks = {}
         parts = {}
+        spent = []
+        quantized = set()
+
+        def slots(i):
+            c, tg, t0 = UNITS[i]
+            w = WIDTHS[c]
+            return [(t0 + s, slice(w * s, w * (s + 1))) for s in range(BANK // w)]
+
+        def product(name, bufs, i, n, operand):
+            c, tg, t0 = UNITS[i]
+            acc = psum.tile([P, BANK], F32, name=name, tag=name, bufs=bufs)
+            for t, cols in slots(i):
+                for lo in range(0, WIDTHS[c], n):
+                    for g in range(PASSES):
+                        codes, plane = operand(g, lo, lo + n)
+                        nc.tensor.matmul_mx(
+                            out=acc[:, cols.start + lo : cols.start + lo + n],
+                            lhsT=x_codes[tg][:, g, t].bitcast(FP8X4),
+                            lhsT_scale=x_plane[tg][:, g, t],
+                            rhs=codes,
+                            rhs_scale=plane,
+                            start=(g == 0),
+                            stop=(g == PASSES - 1),
+                        )
+            banks[name, i] = acc
 
         def gate_product(i):
-            c = i // (PACK * TOKEN_GROUPS)
-            acc = psum.tile([P, N], F32, name="a", tag="a", bufs=2)
+            c = UNITS[i][0]
             product(
-                acc,
-                i,
-                [gate_codes[:, c, g].bitcast(FP8X4) for g in range(PASSES)],
-                [gate_plane[:, c, g] for g in range(PASSES)],
+                "a", 2, i, WIDTHS[c],
+                lambda g, lo, hi: (gate_codes[c][:, g, lo:hi].bitcast(FP8X4), gate_plane[c][:, g, lo:hi]),
             )
-            banks["a", i] = acc
 
-        def up_down_products(i):
-            c = i // (PACK * TOKEN_GROUPS)
-            u = psum.tile([P, N], F32, name="u", tag="u", bufs=3)
+        def up_product(i):
+            c = UNITS[i][0]
             product(
-                u,
-                i,
-                [up_codes[:, c, g].bitcast(FP8X4) for g in range(PASSES)],
-                [up_plane[:, g, N * c : N * (c + 1)] for g in range(PASSES)],
+                "u", 3, i, WIDTHS[c],
+                lambda g, lo, hi: (
+                    up_codes[c][:, g, lo:hi].bitcast(FP8X4),
+                    up_plane[UP_ROW:, g, STARTS[c] + lo : STARTS[c] + hi],
+                ),
             )
-            d = psum.tile([P, N], F32, name="d", tag="d", bufs=3)
+
+        def down_product(i):
+            c = UNITS[i][0]
             product(
-                d,
-                i,
-                [down_codes[:, c, g].bitcast(FP4X4) for g in range(PASSES)],
-                [down_plane[:, g, N * c : N * (c + 1)] for g in range(PASSES)],
+                "d", 3, i, BANK if WIDTHS[c] == BANK else P,
+                lambda g, lo, hi: (
+                    down_codes[c][:, g, 2 * lo : 2 * hi].bitcast(FP4X4),
+                    down_plane[:, g, STARTS[c] + lo : STARTS[c] + hi],
+                ),
             )
-            banks["u", i] = u
-            banks["d", i] = d
 
-        def activations(i):
-            a = banks["a", i]
-            th = work.tile([P, N], F32, name="th", tag="th", bufs=3)
-            nc.scalar.activation(out=th[:], in_=a[:], func=ACT.Tanh, bias=zero_bias[:], scale=C / 2)
-            sn = work.tile([P, N], F32, name="sn", tag="sn", bufs=3)
-            nc.scalar.activation(out=sn[:], in_=a[:], func=ACT.Silu, bias=zero_bias[:], scale=-C)
-            parts["th", i] = th
-            parts["sn", i] = sn
+        def part(name, i):
+            tile = work.tile([P, BANK], F32, name=name, tag=name, bufs=BUFS[name])
+            parts[name, i] = tile
+            return tile
 
-        def drain_products(i):
-            left = work.tile([P, N], F32, name="left", tag="left", bufs=3)
+        def tanh_part(i):
+            nc.scalar.activation(
+                out=part("th", i)[:], in_=banks["a", i][:], func=ACT.Tanh, bias=zero_bias[:], scale=C / 2
+            )
+
+        def silu_part(i):
+            nc.scalar.activation(
+                out=part("sn", i)[:], in_=banks["a", i][:], func=ACT.Silu, bias=zero_bias[:], scale=-C
+            )
+
+        def times_up(i):
             nc.vector.scalar_tensor_tensor(
-                out=left[:], in0=parts["th", i][:], scalar=1.0, in1=banks["u", i][:], op0=ALU.add, op1=ALU.mult
+                out=part("left", i)[:], in0=parts["th", i][:], scalar=1.0, in1=banks["u", i][:],
+                op0=ALU.add, op1=ALU.mult,
             )
-            right = work.tile([P, N], F32, name="right", tag="right", bufs=3)
+
+        def times_down(i):
             nc.vector.scalar_tensor_tensor(
-                out=right[:], in0=parts["sn", i][:], scalar=1.0, in1=banks["d", i][:], op0=ALU.subtract, op1=ALU.mult
+                out=part("right", i)[:], in0=parts["sn", i][:], scalar=1.0, in1=banks["d", i][:],
+                op0=ALU.subtract, op1=ALU.mult,
             )
-            parts["left", i] = left
-            parts["right", i] = right
 
-        def finish(i, lo, hi):
-            j, t = divmod(i, PACK)
-            c, tg = divmod(j, TOKEN_GROUPS)
-            nc.vector.scalar_tensor_tensor(
-                out=y[:, j, t, lo:hi],
-                in0=parts["left", i][:, lo:hi],
-                scalar=factor[:, tg, t : t + 1],
-                in1=parts["right", i][:, lo:hi],
-                op0=ALU.mult,
-                op1=ALU.mult,
+        def left_times_down(i):
+            nc.vector.tensor_tensor(
+                out=part("right", i)[:], in0=parts["left", i][:], in1=banks["d", i][:], op=ALU.mult
             )
-            nc.sync.dma_start(out=y_dst[:, tg, t, N * c + lo : N * c + hi], in_=y[:, j, t, lo:hi])
 
-        nc.vector.memset(xs_raw[:].bitcast(I32), 0)
-        nc.vector.memset(zero_in[:], 0.0)
-        nc.vector.memset(up_plane[:].bitcast(I32), 0)
-        nc.vector.memset(down_plane[:].bitcast(I32), 0)
-        nc.scalar.activation(out=zero_bias[:], in_=zero_in[:], func=ACT.Silu)
-        nc.gpsimd.dma_start(out=rate_raw[:], in_=rate.rearrange("(g p t) o -> p g (t o)", p=P, t=PACK))
-        nc.gpsimd.tensor_scalar(
-            out=factor[:], in0=rate_raw[:], scalar1=-0.5, scalar2=0.0, op0=ALU.mult, op1=ALU.add
-        )
+        def rate_on_gpsimd(i):
+            c, tg, t0 = UNITS[i]
+            if spent:
+                rated = spent[-1]
+                parts["rated", i] = rated
+                spent.clear()
+            else:
+                rated = part("rated", i)
+            for t, cols in slots(i):
+                nc.gpsimd.tensor_scalar(
+                    out=rated[:, cols], in0=parts["sn", i][:, cols],
+                    scalar1=minus_half_rate[:, tg, t : t + 1], scalar2=half_rate[:, tg, t : t + 1],
+                    op0=ALU.mult, op1=ALU.add,
+                )
 
-        load_x(0)
-        load_scale_rows(xs_raw, x_scales)
-        load_gate(0, 0)
-        load_gate(0, 1)
-        load_up_down(0)
-        load_scale_rows(up_plane, up_scales)
-        load_scale_rows(down_plane, down_scales)
-        load_x(1)
-        for c in range(1, CHUNKS):
-            load_gate(c, 0)
-            load_gate(c, 1)
-            load_up_down(c)
+        def unit_rows(i):
+            c, tg, t0 = UNITS[i]
+            return slice(t0, t0 + BANK // WIDTHS[c])
 
-        permute_x_codes(0)
-        permute_x_scales(0)
-        group_gate(True, 0, 0, 0, HEAD_SPLIT)
-        group_gate(False, 0, 0, HEAD_SPLIT, N)
-        group_gate(False, 0, 1, HEAD_SPLIT, N)
-        group_gate(True, 0, 1, 0, HEAD_SPLIT)
-        quantize_gate(0, 0)
-        quantize_gate(0, 1)
-        permute_x_scales(1)
-        permute_x_codes(1)
+        def finish_on_gpsimd(i):
+            c, tg, t0 = UNITS[i]
+            out = y[TOKEN_GROUPS * c + tg][:, unit_rows(i)].rearrange("p t n -> p (t n)")
+            nc.gpsimd.tensor_tensor(out=out, in0=parts["right", i][:], in1=parts["rated", i][:], op=ALU.mult)
 
-        scalar_extra = {
-            1: ("gate", 1, 0, 0), 2: ("gate", 1, 0, 1), 3: ("gate", 1, 1, 0), 4: ("gate", 1, 1, 1),
-            6: ("y", 0, 0), 7: ("y", 0, 1), 8: ("gate", 2, 0, 0), 9: ("gate", 2, 0, 1),
-            11: ("gate", 2, 1, 0), 12: ("gate", 2, 1, 1), 13: ("y", 1, 0), 14: ("y", 1, 1),
-            15: ("y", 2, 0), 17: ("y", 2, 1), 18: ("y", 3, 0), 19: ("y", 3, 1),
-            21: ("y", 4, 0), 22: ("y", 4, 1),
-        }
-        vector_extra = {
-            3: ("gate", 1, 0), 5: ("gate", 1, 1), 8: ("y", 0), 10: ("gate", 2, 0), 13: ("gate", 2, 1),
-            15: ("y", 1), 18: ("y", 2), 20: ("y", 3), 23: ("y", 4),
-        }
+        def finish_on_vector(i):
+            c, tg, t0 = UNITS[i]
+            for t, cols in slots(i):
+                nc.vector.scalar_tensor_tensor(
+                    out=y[TOKEN_GROUPS * c + tg][:, t], in0=parts["left", i][:, cols],
+                    scalar=minus_half_rate[:, tg, t : t + 1], in1=parts["right", i][:, cols],
+                    op0=ALU.mult, op1=ALU.mult,
+                )
+            spent.append(parts["right", i])
 
-        gate_product(0)
-        for i in range(UNITS):
-            if i + 1 < UNITS:
-                gate_product(i + 1)
-            up_down_products(i)
-            activations(i)
-            extra = scalar_extra.get(i)
-            if extra is not None and extra[0] == "gate":
-                group_gate(False, extra[1], extra[2], HALF * extra[3], HALF * (extra[3] + 1))
-            if extra is not None and extra[0] == "y":
-                group_y(False, extra[1], HALF * extra[2], HALF * (extra[2] + 1))
-            drain_products(i)
-            if i > 0:
-                finish(i - 1, 0, N)
-            extra = vector_extra.get(i)
-            if extra is not None and extra[0] == "gate":
-                quantize_gate(extra[1], extra[2])
-            if extra is not None and extra[0] == "y":
-                quantize_y(extra[1], 0, N)
-                if extra[1] % TOKEN_GROUPS == TOKEN_GROUPS - 1:
-                    store_y_scales(extra[1] // TOKEN_GROUPS)
+        def store_y(i):
+            c, tg, t0 = UNITS[i]
+            nc.sync.dma_start(
+                out=y_dst[:, tg, unit_rows(i), STARTS[c] : STARTS[c] + WIDTHS[c]],
+                in_=y[TOKEN_GROUPS * c + tg][:, unit_rows(i)],
+            )
 
-        last = UNITS - 1
-        finish(last, 0, HALF)
-        finish(last, HALF, N)
-        group_y(False, GROUPS - 1, 0, HALF)
-        group_y(True, GROUPS - 1, HALF, N)
-        quantize_y(GROUPS - 1, 0, HALF)
-        quantize_y(GROUPS - 1, HALF, N)
-        store_y_scales(CHUNKS - 1)
+        def step(item):
+            kind = item[0]
+            if kind == "G":
+                group_gate(*item[1:])
+            elif kind == "QG":
+                quantize_gate(*item[1:])
+            elif kind == "Y":
+                group_y(*item[1:])
+            elif kind == "QY":
+                j = item[1]
+                quantize_y(j)
+                store_y_codes(j)
+                quantized.add(j)
+                if j + 1 - 2 * (j % 2) in quantized:
+                    store_y_scales(j // 2)
+            elif kind == "C":
+                finish_on_vector(item[1])
+                store_y(item[1])
+            elif kind == "TS":
+                rate_on_gpsimd(item[1])
+            elif kind == "TT":
+                finish_on_gpsimd(item[1])
+                store_y(item[1])
+            elif kind == "PXS":
+                permute_x_scales(item[1])
+            elif kind == "PXC":
+                permute_x_codes(item[1])
+            elif kind == "PXH":
+                permute_x_pass(item[1])
+            elif kind == "M":
+                (gate_product, up_product, down_product)[item[2]](item[1])
+            elif kind == "ACT":
+                silu_part(item[1])
+                tanh_part(item[1])
+            elif kind == "A":
+                times_up(item[1])
+            elif kind == "B":
+                times_down(item[1])
+            elif kind == "Bp":
+                left_times_down(item[1])
+            elif kind == "Lg":
+                load_gate(*item[1:])
+            elif kind == "Ls":
+                load_scale_rows(*item[1:])
+            elif kind == "Lx":
+                load_x(1)
+            elif kind == "Lh":
+                load_x_pass(item[1])
+            elif kind == "Lu":
+                load_up(item[1])
+            elif kind == "Ld":
+                load_down(item[1])
+            elif kind == "R":
+                scale_rate()
+
+        clear_plane("V", "x")
+        warm_table()
+        clear_plane("V", "up")
+        clear_plane("V", "down")
+        load_rate("G")
+        for item in ORDER:
+            step(item)

@@ -20,47 +20,66 @@ PACK = 4
 SPAN = P * PACK
 PASSES = D // SPAN
 TOKEN_GROUPS = T // SPAN
+QUADRANTS = 4
 BANK = 512
+FP4_NARROW = 128
 UP_ROW = 4
-BUFS = {"sn": 5, "th": 4, "left": 4, "right": 5, "rated": 1}
+
 WIDTHS = [256, 512, 512, 256]
 STARTS = [sum(WIDTHS[:c]) for c in range(len(WIDTHS))]
 CHUNKS = len(WIDTHS)
 GROUPS = CHUNKS * TOKEN_GROUPS
+HALF_F = F // 2
 UNITS = [
     (c, tg, t0)
     for c in range(CHUNKS)
     for tg in range(TOKEN_GROUPS)
     for t0 in range(0, PACK, BANK // WIDTHS[c])
 ]
-ORDER = [
-    ("Lg", 0, 1), ("Ls", "S", "x", 2), ("Lh", 1), ("Lg", 0, 0), ("Ls", "S", "x", 3), ("Lh", 0), ("Ls", "S", "x", 0), ("Ls", "S", "x", 1), ("Ls", "S", "up", 1), ("Lg", 1, 1), ("Ls", "S", "up", 2), ("Lx",), ("Ls", "S", "up", 3), ("Lu", 0), ("Ls", "S", "up", 0), ("Ls", "S", "down", 2), ("Lg", 1, 0), ("Ls", "S", "down", 3), ("Ls", "S", "down", 0), ("Ls", "S", "down", 1), ("Ld", 0), ("Lg", 2, 1), ("Lu", 1), ("Lg", 3, 0), ("Ld", 3), ("Ld", 1), ("Lg", 3, 1), ("Ld", 2), ("Lg", 2, 0), ("Lu", 3), ("Lu", 2), ("R",), ("G", "A", 0, 1, 0, 128), ("G", "V", 0, 1, 128, 256), ("PXH", 1), ("PXS", 0), ("PXH", 0), ("G", "A", 0, 0, 128, 256), ("G", "A", 0, 0, 0, 128), ("QG", 0, 1), ("G", "A", 1, 1, 0, 256), ("QG", 0, 0), ("PXS", 1), ("G", "V", 1, 1, 256, 512), ("PXC", 1), ("QG", 1, 1),
-    ("M", 0, 0), ("M", 1, 0), ("M", 1, 1), ("M", 0, 1), ("ACT", 0), ("ACT", 1), ("G", "A", 1, 0, 256, 512), ("A", 0), ("G", "V", 1, 0, 0, 256),
-    ("M", 2, 0), ("M", 2, 1), ("M", 1, 2), ("M", 0, 2), ("ACT", 2), ("A", 1), ("B", 1), ("Bp", 0), ("QG", 1, 0), ("C", 1), ("G", "V", 2, 1, 256, 512),
-    ("M", 3, 0), ("G", "A", 2, 1, 0, 256), ("ACT", 3), ("TS", 0), ("TT", 0), ("A", 2),
-    ("M", 3, 1), ("M", 2, 2), ("M", 3, 2), ("G", "A", 3, 0, 0, 256), ("A", 3), ("B", 3), ("Bp", 2), ("C", 3), ("Y", "V", 0, 0, 256),
-    ("M", 4, 1), ("M", 4, 0), ("M", 4, 2), ("ACT", 4), ("TS", 2), ("TT", 2), ("A", 4),
-    ("M", 5, 1), ("M", 5, 0), ("M", 5, 2), ("ACT", 5), ("G", "A", 2, 0, 0, 256), ("A", 5), ("B", 5), ("Bp", 4), ("C", 5), ("G", "V", 2, 0, 256, 512),
-    ("M", 6, 1), ("M", 6, 0), ("M", 6, 2), ("ACT", 6), ("TS", 4), ("TT", 4), ("A", 6),
-    ("M", 7, 1), ("M", 7, 0), ("M", 7, 2), ("ACT", 7), ("G", "A", 3, 1, 0, 256), ("A", 7), ("B", 7), ("Bp", 6), ("C", 7), ("QG", 2, 0),
-    ("M", 8, 1), ("M", 8, 0), ("M", 8, 2), ("ACT", 8), ("TS", 6), ("TT", 6), ("A", 8),
-    ("M", 9, 1), ("M", 9, 0), ("M", 9, 2), ("ACT", 9), ("Y", "A", 1, 0, 256), ("A", 9), ("B", 9), ("Bp", 8), ("QG", 2, 1), ("C", 9),
-    ("M", 10, 1), ("M", 10, 0), ("M", 10, 2), ("ACT", 10), ("TS", 8), ("TT", 8), ("A", 10),
-    ("M", 11, 1), ("M", 11, 0), ("M", 11, 2), ("ACT", 11), ("A", 11), ("B", 11), ("Bp", 10), ("QY", 0), ("C", 11), ("QG", 3, 1),
-    ("M", 12, 1), ("M", 12, 0), ("M", 12, 2), ("ACT", 12), ("TS", 10), ("TT", 10), ("A", 12),
-    ("M", 13, 1), ("M", 13, 0), ("M", 13, 2), ("ACT", 13), ("Y", "A", 2, 0, 256), ("A", 13), ("B", 13), ("Bp", 12), ("C", 13), ("QY", 1),
-    ("M", 14, 1), ("M", 14, 0), ("M", 14, 2), ("ACT", 14), ("TS", 12), ("TT", 12), ("A", 14),
-    ("M", 15, 1), ("M", 15, 0), ("M", 15, 2), ("ACT", 15), ("Y", "A", 2, 256, 512), ("A", 15), ("B", 15), ("Bp", 14), ("C", 15), ("Y", "V", 3, 256, 512),
-    ("M", 16, 1), ("M", 16, 0), ("M", 16, 2), ("ACT", 16), ("TS", 14), ("TT", 14), ("A", 16),
-    ("M", 17, 1), ("M", 17, 0), ("M", 17, 2), ("ACT", 17), ("Y", "A", 3, 0, 256), ("A", 17), ("B", 17), ("Bp", 16), ("QG", 3, 0), ("C", 17), ("QY", 2),
-    ("M", 18, 1), ("M", 18, 0), ("M", 18, 2), ("ACT", 18), ("TS", 16), ("TT", 16), ("A", 18),
-    ("M", 19, 1), ("M", 19, 0), ("M", 19, 2), ("ACT", 19), ("Y", "A", 4, 0, 256), ("A", 19), ("B", 19), ("Bp", 18), ("C", 19), ("QY", 3),
-    ("M", 20, 1), ("M", 20, 0), ("M", 20, 2), ("ACT", 20), ("TS", 18), ("TT", 18), ("A", 20),
-    ("M", 21, 1), ("M", 21, 0), ("M", 21, 2), ("ACT", 21), ("Y", "A", 4, 256, 512), ("A", 21), ("B", 21), ("Bp", 20), ("C", 21), ("QY", 4),
-    ("M", 22, 1), ("M", 22, 0), ("M", 22, 2), ("ACT", 22), ("TS", 20), ("A", 22), ("B", 22),
-    ("M", 23, 1), ("M", 23, 0), ("M", 23, 2), ("ACT", 23), ("Y", "A", 5, 0, 256), ("Y", "A", 5, 256, 512), ("TT", 20), ("A", 23), ("B", 23), ("C", 22), ("QY", 5), ("C", 23),
-    ("Y", "A", 6, 0, 256), ("Y", "A", 7, 128, 256), ("Y", "V", 7, 0, 128), ("QY", 6), ("QY", 7),
 
+PSUM_BUFS = {"a": 2, "u": 3, "e": 3}
+PART_BUFS = {"silu": 5, "tanh": 4, "left": 4, "right": 5}
+
+LOADS = [
+    ("gate", 0, 0), ("scales", "x"), ("gate", 0, 1), ("x_pass", 0), ("x_pass", 1), ("gate", 1, 0), ("x_second",),
+    ("scales", "up"), ("up", 0), ("gate", 1, 1), ("scales", "down"), ("down", 0), ("gate", 3, 0), ("up", 1),
+    ("down", 1), ("gate", 2, 0), ("gate", 2, 1), ("gate", 3, 1), ("up", 2), ("down", 2), ("up", 3), ("down", 3),
+]
+
+HEAD = [
+    ("group_gate", "scalar", 0, 0, 0, 128), ("group_gate", "vector", 0, 0, 128, 256), ("order_x_scales", 0),
+    ("group_gate", "scalar", 0, 1, 0, 128), ("group_gate", "scalar", 0, 1, 128, 256), ("order_x_pass", 0),
+    ("quantize_gate", 0, 0), ("order_x_pass", 1), ("quantize_gate", 0, 1), ("order_x_scales", 1),
+    ("group_gate", "vector", 1, 0, 0, 256), ("group_gate", "vector", 1, 0, 256, 512), ("order_x_second",),
+    ("quantize_gate", 1, 0),
+]
+
+FIRST_PRODUCTS = {
+    0: [("a", 0), ("a", 1), ("u", 0), ("u", 1)],
+    1: [("u", 2), ("a", 2), ("e", 1), ("e", 0)],
+    2: [],
+    3: [("a", 3), ("u", 3), ("e", 3), ("e", 2)],
+}
+
+SCALAR_AFTER_ACTIVATIONS = {
+    1: ("group_gate", "scalar", 1, 1, 0, 256), 2: ("group_gate", "scalar", 3, 0, 0, 256),
+    3: ("group_gate", "scalar", 2, 0, 0, 256), 5: ("group_y", "scalar", 0, 0, 256),
+    7: ("group_gate", "scalar", 2, 1, 0, 256), 9: ("group_gate", "scalar", 3, 1, 0, 256),
+    11: ("group_y", "scalar", 1, 0, 256), 13: ("group_y", "scalar", 2, 0, 256),
+    15: ("group_y", "scalar", 2, 256, 512), 17: ("group_y", "scalar", 3, 0, 256),
+    19: ("group_y", "scalar", 3, 256, 512), 21: ("group_y", "scalar", 4, 0, 256),
+    23: ("group_y", "scalar", 4, 256, 512),
+}
+VECTOR_AFTER_PSUM_READS = {0: ("group_gate", "vector", 1, 1, 256, 512), 13: ("quantize_y", 0)}
+VECTOR_AFTER_FINISH = {
+    1: ("quantize_gate", 1, 1), 3: ("group_gate", "vector", 2, 0, 256, 512),
+    5: ("group_gate", "vector", 2, 1, 256, 512), 7: ("quantize_gate", 2, 0), 9: ("quantize_gate", 2, 1),
+    11: ("quantize_gate", 3, 0), 13: ("quantize_gate", 3, 1), 15: ("quantize_y", 1), 17: ("quantize_y", 2),
+    19: ("quantize_y", 3), 21: ("group_y", "vector", 5, 256, 512),
+}
+TAIL = [
+    ("group_y", "scalar", 5, 0, 256), ("group_y", "scalar", 6, 0, 256), ("quantize_y", 4), ("quantize_y", 5),
+    ("group_y", "scalar", 7, 0, 256), ("quantize_y", 6), ("quantize_y", 7),
 ]
 
 
@@ -70,8 +89,8 @@ def tile_geglu_recompute_gate_descent_k3_kernel(
     nc = tc.nc
     with ExitStack() as ctx:
         keep = ctx.enter_context(tc.tile_pool(name="keep", bufs=1))
-        work = ctx.enter_context(tc.tile_pool(name="work", bufs=3))
-        psum = ctx.enter_context(tc.psum_pool(name="psum", bufs=2))
+        work = ctx.enter_context(tc.tile_pool(name="work", bufs=1))
+        psum = ctx.enter_context(tc.psum_pool(name="psum", bufs=1))
         ctx.enter_context(tc.manual_schedule())
 
         def kept(name, shape, dtype):
@@ -79,7 +98,7 @@ def tile_geglu_recompute_gate_descent_k3_kernel(
 
         x_raw = [kept("x_raw%d" % tg, [P, PASSES, SPAN], I32) for tg in range(TOKEN_GROUPS)]
         x_codes = [kept("x_codes%d" % tg, [P, PASSES, PACK, P], I32) for tg in range(TOKEN_GROUPS)]
-        xs_raw = kept("xs_raw", [P, PASSES, T], U8)
+        x_plane_raw = kept("x_plane_raw", [P, PASSES, T], U8)
         x_plane = [kept("x_plane%d" % tg, [P, PASSES, PACK, P], U8) for tg in range(TOKEN_GROUPS)]
         gate_raw = [kept("gate_raw%d" % c, [P, PASSES, PACK, w], BF16) for c, w in enumerate(WIDTHS)]
         gate_grouped = [kept("gate_grouped%d" % c, [P, PASSES, w, PACK], BF16) for c, w in enumerate(WIDTHS)]
@@ -94,62 +113,46 @@ def tile_geglu_recompute_gate_descent_k3_kernel(
         half_rate = kept("half_rate", [P, TOKEN_GROUPS, PACK], F32)
         zero_in = kept("zero_in", [P, 1], F32)
         zero_bias = kept("zero_bias", [P, 1], F32)
-        group_width = [WIDTHS[j // TOKEN_GROUPS] for j in range(GROUPS)]
-        y = [kept("y%d" % j, [P, PACK, w], F32) for j, w in enumerate(group_width)]
-        y_grouped = [kept("y_grouped%d" % j, [P, w, PACK], BF16) for j, w in enumerate(group_width)]
-        y_codes = [kept("y_codes%d" % j, [P, w], I32) for j, w in enumerate(group_width)]
-        y_plane = [kept("y_plane%d" % c, [P, TOKEN_GROUPS, w], U8) for c, w in enumerate(WIDTHS)]
+        y = [kept("y%d" % j, [P, PACK, WIDTHS[j // TOKEN_GROUPS]], F32) for j in range(GROUPS)]
+        y_grouped = [kept("y_grouped%d" % j, [P, WIDTHS[j // TOKEN_GROUPS], PACK], BF16) for j in range(GROUPS)]
+        y_codes = [kept("y_codes%d" % c, [P, TOKEN_GROUPS, w], I32) for c, w in enumerate(WIDTHS)]
+        y_plane = [kept("y_plane%d" % h, [P, TOKEN_GROUPS, HALF_F], U8) for h in range(F // HALF_F)]
 
         x_src = x_words.rearrange("g p n t -> p g (n t)").bitcast(I32)
         up_src = up_words.rearrange("g p n t -> p g (n t)").bitcast(I32)
         down_src = down_words.rearrange("g p b -> p g b").bitcast(I32)
         codes_dst = out_1.rearrange("g p n t -> p g (n t)").bitcast(I32)
         y_dst = out_0.rearrange("(g p t) n -> p g t n", p=P, t=PACK)
-        planes = {"x": (xs_raw, x_scales), "up": (up_plane, up_scales), "down": (down_plane, down_scales)}
-        engines = {"V": nc.vector, "G": nc.gpsimd, "S": nc.sync, "A": nc.scalar}
+        loaded_planes = {
+            "x": (x_plane_raw, x_scales, 0),
+            "up": (up_plane, up_scales, UP_ROW),
+            "down": (down_plane, down_scales, 0),
+        }
 
-        def clear_plane(engine, name):
-            engines[engine].memset(planes[name][0][:].bitcast(I32), 0)
+        def chunk_cols(c):
+            return slice(STARTS[c], STARTS[c] + WIDTHS[c])
 
-        def load_scale_rows(engine, name, q):
-            plane, scales = planes[name]
-            row = 32 * q + (UP_ROW if name == "up" else 0)
-            engines[engine].dma_start(
-                out=plane[:].bitcast(I32)[row : row + 4],
-                in_=scales.bitcast(I32)[:, 4 * q : 4 * q + 4, :].rearrange("g r n -> r g n"),
-            )
-
-        def warm_table():
-            nc.vector.memset(zero_in[:], 0.0)
-            nc.scalar.activation(out=zero_bias[:], in_=zero_in[:], func=ACT.Silu)
-
-        def load_rate(engine):
-            engines[engine].dma_start(out=rate_raw[:], in_=rate.rearrange("(g p t) o -> p g (t o)", p=P, t=PACK))
-
-        def scale_rate():
-            for dst, by in ((minus_half_rate, -0.5), (half_rate, 0.5)):
-                nc.gpsimd.tensor_scalar(
-                    out=dst[:], in0=rate_raw[:], scalar1=by, scalar2=0.0, op0=ALU.mult, op1=ALU.add
+        def load_scales(name):
+            plane, scales, first_row = loaded_planes[name]
+            for q in range(QUADRANTS):
+                row = 32 * q + first_row
+                nc.sync.dma_start(
+                    out=plane[:].bitcast(I32)[row : row + 4],
+                    in_=scales.bitcast(I32)[:, 4 * q : 4 * q + 4, :].rearrange("g r n -> r g n"),
                 )
-
-        def load_x(tg):
-            nc.sync.dma_start(out=x_raw[tg][:], in_=x_src[:, :, SPAN * tg : SPAN * (tg + 1)])
 
         def load_x_pass(g):
             nc.sync.dma_start(out=x_raw[0][:, g], in_=x_src[:, g, 0:SPAN])
 
-        def permute_x_pass(g):
-            nc.vector.tensor_copy(
-                out=x_codes[0][:, g].rearrange("p t m -> p m t"),
-                in_=x_raw[0][:, g].rearrange("p (m t) -> p m t", t=PACK),
-            )
+        def load_x_second():
+            nc.sync.dma_start(out=x_raw[1][:], in_=x_src[:, :, SPAN : 2 * SPAN])
 
         def load_gate(c, g):
-            rows = w_gate[SPAN * g : SPAN * (g + 1), STARTS[c] : STARTS[c] + WIDTHS[c]]
+            rows = w_gate[SPAN * g : SPAN * (g + 1), chunk_cols(c)]
             nc.sync.dma_start(out=gate_raw[c][:, g], in_=rows.rearrange("(p j) n -> p j n", j=PACK))
 
         def load_up(c):
-            nc.sync.dma_start(out=up_codes[c][:], in_=up_src[:, :, STARTS[c] : STARTS[c] + WIDTHS[c]])
+            nc.sync.dma_start(out=up_codes[c][:], in_=up_src[:, :, chunk_cols(c)])
 
         def load_down(c):
             nc.sync.dma_start(
@@ -157,27 +160,29 @@ def tile_geglu_recompute_gate_descent_k3_kernel(
                 in_=down_src[:, :, STARTS[c] // 2 : (STARTS[c] + WIDTHS[c]) // 2],
             )
 
-        def permute_x_codes(tg):
+        def order_x_pass(g):
             nc.vector.tensor_copy(
-                out=x_codes[tg][:].rearrange("p g t m -> p g m t"),
-                in_=x_raw[tg][:].rearrange("p g (m t) -> p g m t", t=PACK),
+                out=x_codes[0][:, g].rearrange("p t m -> p m t"),
+                in_=x_raw[0][:, g].rearrange("p (m t) -> p m t", t=PACK),
             )
 
-        def permute_x_scales(tg):
+        def order_x_second():
+            nc.vector.tensor_copy(
+                out=x_codes[1][:].rearrange("p g t m -> p g m t"),
+                in_=x_raw[1][:].rearrange("p g (m t) -> p g m t", t=PACK),
+            )
+
+        def order_x_scales(tg):
             nc.vector.tensor_copy(
                 out=x_plane[tg][:],
-                in_=xs_raw[:, :, SPAN * tg : SPAN * (tg + 1)].rearrange("p g (m t) -> p g t m", t=PACK),
+                in_=x_plane_raw[:, :, SPAN * tg : SPAN * (tg + 1)].rearrange("p g (m t) -> p g t m", t=PACK),
             )
 
         def interleave(engine, dst, src, run):
             out = dst.rearrange("p (c i) t -> p c t i", i=run)
             in_ = src.rearrange("p t (c i) -> p c t i", i=run)
-            if engine == "V":
+            if engine == "vector":
                 nc.vector.tensor_copy(out=out, in_=in_)
-            elif engine == "G":
-                nc.gpsimd.tensor_scalar(
-                    out=dst, in0=src.rearrange("p t n -> p n t"), scalar1=1.0, scalar2=-0.0, op0=ALU.mult, op1=ALU.add
-                )
             else:
                 nc.scalar.copy(out=out, in_=in_)
 
@@ -194,43 +199,54 @@ def tile_geglu_recompute_gate_descent_k3_kernel(
         def group_y(engine, j, lo, hi):
             interleave(engine, y_grouped[j][:, lo:hi, :], y[j][:, :, lo:hi], 2)
 
+        def store_y_scales(h):
+            cols = slice(h * HALF_F // 4, (h + 1) * HALF_F // 4)
+            for q in range(QUADRANTS):
+                queue = nc.scalar if h == len(y_plane) - 1 and q % 2 == 1 else nc.sync
+                queue.dma_start(
+                    out=out_2.bitcast(I32)[:, 4 * q : 4 * q + 4, cols].rearrange("g r n -> r g n"),
+                    in_=y_plane[h][:].bitcast(I32)[32 * q : 32 * q + 4],
+                )
+
         def quantize_y(j):
             c, tg = divmod(j, TOKEN_GROUPS)
+            h, lo = divmod(STARTS[c], HALF_F)
             nc.vector.quantize_mx(
-                out=y_codes[j][:].bitcast(FP8X4),
-                scales=y_plane[c][:, tg],
+                out=y_codes[c][:, tg].bitcast(FP8X4),
+                scales=y_plane[h][:, tg, lo : lo + WIDTHS[c]],
                 in_=y_grouped[j][:].rearrange("p n t -> p (n t)"),
             )
-
-        def store_y_codes(j):
-            c, tg = divmod(j, TOKEN_GROUPS)
-            nc.sync.dma_start(out=codes_dst[:, tg, STARTS[c] : STARTS[c] + WIDTHS[c]], in_=y_codes[j][:])
-
-        def store_y_scales(c):
-            cols = slice(STARTS[c] // 4, (STARTS[c] + WIDTHS[c]) // 4)
-            for q in range(4):
-                nc.sync.dma_start(
-                    out=out_2.bitcast(I32)[:, 4 * q : 4 * q + 4, cols].rearrange("g r n -> r g n"),
-                    in_=y_plane[c][:].bitcast(I32)[32 * q : 32 * q + 4],
-                )
+            if c < CHUNKS - 1:
+                nc.sync.dma_start(out=codes_dst[:, tg, chunk_cols(c)], in_=y_codes[c][:, tg])
+            elif tg == TOKEN_GROUPS - 1:
+                nc.sync.dma_start(out=codes_dst[:, :, chunk_cols(c)], in_=y_codes[c][:])
+            if tg == TOKEN_GROUPS - 1 and lo + WIDTHS[c] == HALF_F:
+                store_y_scales(h)
 
         banks = {}
         parts = {}
-        spent = []
-        quantized = set()
 
-        def slots(i):
+        def slices_of(i):
             c, tg, t0 = UNITS[i]
             w = WIDTHS[c]
             return [(t0 + s, slice(w * s, w * (s + 1))) for s in range(BANK // w)]
 
-        def product(name, bufs, i, n, operand):
+        def moving_operand(name, c, g, lo, hi):
+            if name == "a":
+                return gate_codes[c][:, g, lo:hi].bitcast(FP8X4), gate_plane[c][:, g, lo:hi]
+            cols = slice(STARTS[c] + lo, STARTS[c] + hi)
+            if name == "u":
+                return up_codes[c][:, g, lo:hi].bitcast(FP8X4), up_plane[UP_ROW:, g, cols]
+            return down_codes[c][:, g, 2 * lo : 2 * hi].bitcast(FP4X4), down_plane[:, g, cols]
+
+        def product(name, i):
             c, tg, t0 = UNITS[i]
-            acc = psum.tile([P, BANK], F32, name=name, tag=name, bufs=bufs)
-            for t, cols in slots(i):
+            n = FP4_NARROW if name == "e" and WIDTHS[c] < BANK else WIDTHS[c]
+            acc = psum.tile([P, BANK], F32, name=name, tag=name, bufs=PSUM_BUFS[name])
+            for t, cols in slices_of(i):
                 for lo in range(0, WIDTHS[c], n):
                     for g in range(PASSES):
-                        codes, plane = operand(g, lo, lo + n)
+                        codes, plane = moving_operand(name, c, g, lo, lo + n)
                         nc.tensor.matmul_mx(
                             out=acc[:, cols.start + lo : cols.start + lo + n],
                             lhsT=x_codes[tg][:, g, t].bitcast(FP8X4),
@@ -242,165 +258,117 @@ def tile_geglu_recompute_gate_descent_k3_kernel(
                         )
             banks[name, i] = acc
 
-        def gate_product(i):
-            c = UNITS[i][0]
-            product(
-                "a", 2, i, WIDTHS[c],
-                lambda g, lo, hi: (gate_codes[c][:, g, lo:hi].bitcast(FP8X4), gate_plane[c][:, g, lo:hi]),
-            )
-
-        def up_product(i):
-            c = UNITS[i][0]
-            product(
-                "u", 3, i, WIDTHS[c],
-                lambda g, lo, hi: (
-                    up_codes[c][:, g, lo:hi].bitcast(FP8X4),
-                    up_plane[UP_ROW:, g, STARTS[c] + lo : STARTS[c] + hi],
-                ),
-            )
-
-        def down_product(i):
-            c = UNITS[i][0]
-            product(
-                "d", 3, i, BANK if WIDTHS[c] == BANK else P,
-                lambda g, lo, hi: (
-                    down_codes[c][:, g, 2 * lo : 2 * hi].bitcast(FP4X4),
-                    down_plane[:, g, STARTS[c] + lo : STARTS[c] + hi],
-                ),
-            )
-
         def part(name, i):
-            tile = work.tile([P, BANK], F32, name=name, tag=name, bufs=BUFS[name])
-            parts[name, i] = tile
-            return tile
+            parts[name, i] = work.tile([P, BANK], F32, name=name, tag=name, bufs=PART_BUFS[name])
+            return parts[name, i]
 
-        def tanh_part(i):
-            nc.scalar.activation(
-                out=part("th", i)[:], in_=banks["a", i][:], func=ACT.Tanh, bias=zero_bias[:], scale=C / 2
-            )
+        def activations(i):
+            a = banks["a", i]
+            nc.scalar.activation(out=part("silu", i)[:], in_=a[:], func=ACT.Silu, bias=zero_bias[:], scale=-C)
+            nc.scalar.activation(out=part("tanh", i)[:], in_=a[:], func=ACT.Tanh, bias=zero_bias[:], scale=C / 2)
 
-        def silu_part(i):
-            nc.scalar.activation(
-                out=part("sn", i)[:], in_=banks["a", i][:], func=ACT.Silu, bias=zero_bias[:], scale=-C
-            )
-
-        def times_up(i):
+        def left_factor(i):
             nc.vector.scalar_tensor_tensor(
-                out=part("left", i)[:], in0=parts["th", i][:], scalar=1.0, in1=banks["u", i][:],
+                out=part("left", i)[:], in0=parts["tanh", i][:], scalar=1.0, in1=banks["u", i][:],
                 op0=ALU.add, op1=ALU.mult,
             )
 
-        def times_down(i):
+        def right_factor(i):
             nc.vector.scalar_tensor_tensor(
-                out=part("right", i)[:], in0=parts["sn", i][:], scalar=1.0, in1=banks["d", i][:],
+                out=part("right", i)[:], in0=parts["silu", i][:], scalar=1.0, in1=banks["e", i][:],
                 op0=ALU.subtract, op1=ALU.mult,
             )
 
-        def left_times_down(i):
+        def left_times_e(i):
             nc.vector.tensor_tensor(
-                out=part("right", i)[:], in0=parts["left", i][:], in1=banks["d", i][:], op=ALU.mult
+                out=part("right", i)[:], in0=parts["left", i][:], in1=banks["e", i][:], op=ALU.mult
             )
 
-        def rate_on_gpsimd(i):
+        def store_y(i):
             c, tg, t0 = UNITS[i]
-            if spent:
-                rated = spent[-1]
-                parts["rated", i] = rated
-                spent.clear()
-            else:
-                rated = part("rated", i)
-            for t, cols in slots(i):
-                nc.gpsimd.tensor_scalar(
-                    out=rated[:, cols], in0=parts["sn", i][:, cols],
-                    scalar1=minus_half_rate[:, tg, t : t + 1], scalar2=half_rate[:, tg, t : t + 1],
-                    op0=ALU.mult, op1=ALU.add,
-                )
-
-        def unit_rows(i):
-            c, tg, t0 = UNITS[i]
-            return slice(t0, t0 + BANK // WIDTHS[c])
-
-        def finish_on_gpsimd(i):
-            c, tg, t0 = UNITS[i]
-            out = y[TOKEN_GROUPS * c + tg][:, unit_rows(i)].rearrange("p t n -> p (t n)")
-            nc.gpsimd.tensor_tensor(out=out, in0=parts["right", i][:], in1=parts["rated", i][:], op=ALU.mult)
+            rows = slice(t0, t0 + BANK // WIDTHS[c])
+            nc.sync.dma_start(out=y_dst[:, tg, rows, chunk_cols(c)], in_=y[TOKEN_GROUPS * c + tg][:, rows])
 
         def finish_on_vector(i):
             c, tg, t0 = UNITS[i]
-            for t, cols in slots(i):
+            for t, cols in slices_of(i):
                 nc.vector.scalar_tensor_tensor(
                     out=y[TOKEN_GROUPS * c + tg][:, t], in0=parts["left", i][:, cols],
                     scalar=minus_half_rate[:, tg, t : t + 1], in1=parts["right", i][:, cols],
                     op0=ALU.mult, op1=ALU.mult,
                 )
-            spent.append(parts["right", i])
+            store_y(i)
 
-        def store_y(i):
+        def finish_on_gpsimd(i):
             c, tg, t0 = UNITS[i]
-            nc.sync.dma_start(
-                out=y_dst[:, tg, unit_rows(i), STARTS[c] : STARTS[c] + WIDTHS[c]],
-                in_=y[TOKEN_GROUPS * c + tg][:, unit_rows(i)],
+            rated = parts["right", i + 1]
+            for t, cols in slices_of(i):
+                nc.gpsimd.tensor_scalar(
+                    out=rated[:, cols], in0=parts["silu", i][:, cols],
+                    scalar1=minus_half_rate[:, tg, t : t + 1], scalar2=half_rate[:, tg, t : t + 1],
+                    op0=ALU.mult, op1=ALU.add,
+                )
+            rows = slice(t0, t0 + BANK // WIDTHS[c])
+            nc.gpsimd.tensor_tensor(
+                out=y[TOKEN_GROUPS * c + tg][:, rows].rearrange("p t n -> p (t n)"),
+                in0=parts["right", i][:], in1=rated[:], op=ALU.mult,
             )
+            store_y(i)
 
-        def step(item):
-            kind = item[0]
-            if kind == "G":
-                group_gate(*item[1:])
-            elif kind == "QG":
-                quantize_gate(*item[1:])
-            elif kind == "Y":
-                group_y(*item[1:])
-            elif kind == "QY":
-                j = item[1]
-                quantize_y(j)
-                store_y_codes(j)
-                quantized.add(j)
-                if j + 1 - 2 * (j % 2) in quantized:
-                    store_y_scales(j // 2)
-            elif kind == "C":
-                finish_on_vector(item[1])
-                store_y(item[1])
-            elif kind == "TS":
-                rate_on_gpsimd(item[1])
-            elif kind == "TT":
-                finish_on_gpsimd(item[1])
-                store_y(item[1])
-            elif kind == "PXS":
-                permute_x_scales(item[1])
-            elif kind == "PXC":
-                permute_x_codes(item[1])
-            elif kind == "PXH":
-                permute_x_pass(item[1])
-            elif kind == "M":
-                (gate_product, up_product, down_product)[item[2]](item[1])
-            elif kind == "ACT":
-                silu_part(item[1])
-                tanh_part(item[1])
-            elif kind == "A":
-                times_up(item[1])
-            elif kind == "B":
-                times_down(item[1])
-            elif kind == "Bp":
-                left_times_down(item[1])
-            elif kind == "Lg":
-                load_gate(*item[1:])
-            elif kind == "Ls":
-                load_scale_rows(*item[1:])
-            elif kind == "Lx":
-                load_x(1)
-            elif kind == "Lh":
-                load_x_pass(item[1])
-            elif kind == "Lu":
-                load_up(item[1])
-            elif kind == "Ld":
-                load_down(item[1])
-            elif kind == "R":
-                scale_rate()
+        steps = {
+            "scales": load_scales, "x_pass": load_x_pass, "x_second": load_x_second, "gate": load_gate,
+            "up": load_up, "down": load_down, "order_x_pass": order_x_pass, "order_x_second": order_x_second,
+            "order_x_scales": order_x_scales, "group_gate": group_gate, "quantize_gate": quantize_gate,
+            "group_y": group_y, "quantize_y": quantize_y,
+        }
 
-        clear_plane("V", "x")
-        warm_table()
-        clear_plane("V", "up")
-        clear_plane("V", "down")
-        load_rate("G")
-        for item in ORDER:
-            step(item)
+        def run(step):
+            steps[step[0]](*step[1:])
+
+        def run_listed(table, i):
+            if i in table:
+                run(table[i])
+
+        def products_and_activations(i):
+            for name, unit in FIRST_PRODUCTS.get(i, [("u", i), ("a", i), ("e", i)]):
+                product(name, unit)
+            activations(i)
+            run_listed(SCALAR_AFTER_ACTIVATIONS, i)
+
+        nc.vector.memset(x_plane_raw[:].bitcast(I32), 0)
+        nc.vector.memset(zero_in[:], 0.0)
+        nc.scalar.activation(out=zero_bias[:], in_=zero_in[:], func=ACT.Silu)
+        nc.vector.memset(up_plane[:].bitcast(I32), 0)
+        nc.vector.memset(down_plane[:].bitcast(I32), 0)
+        nc.gpsimd.dma_start(out=rate_raw[:], in_=rate.rearrange("(g p t) o -> p g (t o)", p=P, t=PACK))
+        for step in LOADS:
+            run(step)
+        for scaled, by in ((minus_half_rate, -0.5), (half_rate, 0.5)):
+            nc.gpsimd.tensor_scalar(
+                out=scaled[:], in0=rate_raw[:], scalar1=by, scalar2=0.0, op0=ALU.mult, op1=ALU.add
+            )
+        for step in HEAD:
+            run(step)
+
+        last_pair = len(UNITS) - 2
+        for first in range(0, len(UNITS), 2):
+            second = first + 1
+            products_and_activations(first)
+            if first > 0:
+                finish_on_gpsimd(first - 2)
+            left_factor(first)
+            if first == last_pair:
+                right_factor(first)
+            run_listed(VECTOR_AFTER_PSUM_READS, first)
+            products_and_activations(second)
+            left_factor(second)
+            right_factor(second)
+            if first == last_pair:
+                finish_on_vector(first)
+            else:
+                left_times_e(first)
+            run_listed(VECTOR_AFTER_PSUM_READS, second)
+            finish_on_vector(second)
+            run_listed(VECTOR_AFTER_FINISH, second)
+        for step in TAIL:
+            run(step)

@@ -20,7 +20,8 @@ PACK = 4
 SPAN = P * PACK
 PASSES = D // SPAN
 TOKEN_GROUPS = T // SPAN
-QUADRANTS = 4
+QUADRANT = 32
+ROWS = 4
 BANK = 512
 FP4_NARROW = 128
 UP_ROW = 4
@@ -29,7 +30,8 @@ WIDTHS = [256, 512, 512, 256]
 STARTS = [sum(WIDTHS[:c]) for c in range(len(WIDTHS))]
 CHUNKS = len(WIDTHS)
 GROUPS = CHUNKS * TOKEN_GROUPS
-HALF_F = F // 2
+HALVES = 2
+HALF_F = F // HALVES
 UNITS = [
     (c, tg, t0)
     for c in range(CHUNKS)
@@ -41,9 +43,10 @@ PSUM_BUFS = {"a": 2, "u": 3, "e": 3}
 PART_BUFS = {"silu": 5, "tanh": 4, "left": 4, "right": 5}
 
 LOADS = [
-    ("gate", 0, 0), ("scales", "x"), ("gate", 0, 1), ("x_pass", 0), ("x_pass", 1), ("gate", 1, 0), ("x_second",),
-    ("scales", "up"), ("up", 0), ("gate", 1, 1), ("scales", "down"), ("down", 0), ("gate", 3, 0), ("up", 1),
-    ("down", 1), ("gate", 2, 0), ("gate", 2, 1), ("gate", 3, 1), ("up", 2), ("down", 2), ("up", 3), ("down", 3),
+    ("gate", 0, 0), ("x_scales",), ("gate", 0, 1), ("x_pass", 0), ("x_pass", 1), ("gate", 1, 0), ("x_second",),
+    ("up_scales", 0), ("up", 0), ("gate", 1, 1), ("down_scales", 0), ("down", 0), ("gate", 3, 0), ("up", 1),
+    ("down", 1), ("gate", 2, 0), ("gate", 2, 1), ("gate", 3, 1), ("up_scales", 1), ("down_scales", 1),
+    ("up", 2), ("down", 2), ("up", 3), ("down", 3),
 ]
 
 HEAD = [
@@ -105,9 +108,9 @@ def tile_geglu_recompute_gate_descent_k3_kernel(
         gate_codes = [kept("gate_codes%d" % c, [P, PASSES, w], I32) for c, w in enumerate(WIDTHS)]
         gate_plane = [kept("gate_plane%d" % c, [P, PASSES, w], U8) for c, w in enumerate(WIDTHS)]
         up_codes = [kept("up_codes%d" % c, [P, PASSES, w], I32) for c, w in enumerate(WIDTHS)]
-        up_plane = kept("up_plane", [P, PASSES, F], U8)
+        up_plane = [kept("up_plane%d" % h, [P, PASSES, HALF_F], U8) for h in range(HALVES)]
         down_codes = [kept("down_codes%d" % c, [P, PASSES, 2 * w], U8) for c, w in enumerate(WIDTHS)]
-        down_plane = kept("down_plane", [P, PASSES, F], U8)
+        down_plane = [kept("down_plane%d" % h, [P, PASSES, HALF_F], U8) for h in range(HALVES)]
         rate_raw = kept("rate_raw", [P, TOKEN_GROUPS, PACK], BF16)
         minus_half_rate = kept("minus_half_rate", [P, TOKEN_GROUPS, PACK], F32)
         half_rate = kept("half_rate", [P, TOKEN_GROUPS, PACK], F32)
@@ -116,30 +119,35 @@ def tile_geglu_recompute_gate_descent_k3_kernel(
         y = [kept("y%d" % j, [P, PACK, WIDTHS[j // TOKEN_GROUPS]], F32) for j in range(GROUPS)]
         y_grouped = [kept("y_grouped%d" % j, [P, WIDTHS[j // TOKEN_GROUPS], PACK], BF16) for j in range(GROUPS)]
         y_codes = [kept("y_codes%d" % c, [P, TOKEN_GROUPS, w], I32) for c, w in enumerate(WIDTHS)]
-        y_plane = [kept("y_plane%d" % h, [P, TOKEN_GROUPS, HALF_F], U8) for h in range(F // HALF_F)]
+        y_plane = [kept("y_plane%d" % h, [P, TOKEN_GROUPS, HALF_F], U8) for h in range(HALVES)]
 
         x_src = x_words.rearrange("g p n t -> p g (n t)").bitcast(I32)
         up_src = up_words.rearrange("g p n t -> p g (n t)").bitcast(I32)
         down_src = down_words.rearrange("g p b -> p g b").bitcast(I32)
         codes_dst = out_1.rearrange("g p n t -> p g (n t)").bitcast(I32)
         y_dst = out_0.rearrange("(g p t) n -> p g t n", p=P, t=PACK)
-        loaded_planes = {
-            "x": (x_plane_raw, x_scales, 0),
-            "up": (up_plane, up_scales, UP_ROW),
-            "down": (down_plane, down_scales, 0),
-        }
 
         def chunk_cols(c):
             return slice(STARTS[c], STARTS[c] + WIDTHS[c])
 
-        def load_scales(name):
-            plane, scales, first_row = loaded_planes[name]
-            for q in range(QUADRANTS):
-                row = 32 * q + first_row
-                nc.sync.dma_start(
-                    out=plane[:].bitcast(I32)[row : row + 4],
-                    in_=scales.bitcast(I32)[:, 4 * q : 4 * q + 4, :].rearrange("g r n -> r g n"),
-                )
+        def half_words(h):
+            return slice(h * HALF_F // 4, (h + 1) * HALF_F // 4)
+
+        def scale_rows(scales, r):
+            return scales.bitcast(I32)[:, r::ROWS, :].rearrange("g q n -> q g n")
+
+        def load_scales(plane, rows_of, first_row):
+            for r in range(ROWS):
+                nc.sync.dma_start(out=plane.bitcast(I32)[first_row + r :: QUADRANT], in_=rows_of(r))
+
+        def load_x_scales():
+            load_scales(x_plane_raw[:], lambda r: scale_rows(x_scales, r), 0)
+
+        def load_up_scales(h):
+            load_scales(up_plane[h][:], lambda r: scale_rows(up_scales, r)[:, :, half_words(h)], UP_ROW)
+
+        def load_down_scales(h):
+            load_scales(down_plane[h][:], lambda r: scale_rows(down_scales, r)[:, :, half_words(h)], 0)
 
         def load_x_pass(g):
             nc.sync.dma_start(out=x_raw[0][:, g], in_=x_src[:, g, 0:SPAN])
@@ -200,12 +208,10 @@ def tile_geglu_recompute_gate_descent_k3_kernel(
             interleave(engine, y_grouped[j][:, lo:hi, :], y[j][:, :, lo:hi], 2)
 
         def store_y_scales(h):
-            cols = slice(h * HALF_F // 4, (h + 1) * HALF_F // 4)
-            for q in range(QUADRANTS):
-                queue = nc.scalar if h == len(y_plane) - 1 and q % 2 == 1 else nc.sync
+            for r in range(ROWS):
+                queue = nc.scalar if h == HALVES - 1 and r % 2 == 1 else nc.sync
                 queue.dma_start(
-                    out=out_2.bitcast(I32)[:, 4 * q : 4 * q + 4, cols].rearrange("g r n -> r g n"),
-                    in_=y_plane[h][:].bitcast(I32)[32 * q : 32 * q + 4],
+                    out=scale_rows(out_2, r)[:, :, half_words(h)], in_=y_plane[h][:].bitcast(I32)[r::QUADRANT]
                 )
 
         def quantize_y(j):
@@ -234,10 +240,11 @@ def tile_geglu_recompute_gate_descent_k3_kernel(
         def moving_operand(name, c, g, lo, hi):
             if name == "a":
                 return gate_codes[c][:, g, lo:hi].bitcast(FP8X4), gate_plane[c][:, g, lo:hi]
-            cols = slice(STARTS[c] + lo, STARTS[c] + hi)
+            h, start = divmod(STARTS[c], HALF_F)
+            cols = slice(start + lo, start + hi)
             if name == "u":
-                return up_codes[c][:, g, lo:hi].bitcast(FP8X4), up_plane[UP_ROW:, g, cols]
-            return down_codes[c][:, g, 2 * lo : 2 * hi].bitcast(FP4X4), down_plane[:, g, cols]
+                return up_codes[c][:, g, lo:hi].bitcast(FP8X4), up_plane[h][UP_ROW:, g, cols]
+            return down_codes[c][:, g, 2 * lo : 2 * hi].bitcast(FP4X4), down_plane[h][:, g, cols]
 
         def product(name, i):
             c, tg, t0 = UNITS[i]
@@ -316,7 +323,8 @@ def tile_geglu_recompute_gate_descent_k3_kernel(
             store_y(i)
 
         steps = {
-            "scales": load_scales, "x_pass": load_x_pass, "x_second": load_x_second, "gate": load_gate,
+            "x_scales": load_x_scales, "up_scales": load_up_scales, "down_scales": load_down_scales,
+            "x_pass": load_x_pass, "x_second": load_x_second, "gate": load_gate,
             "up": load_up, "down": load_down, "order_x_pass": order_x_pass, "order_x_second": order_x_second,
             "order_x_scales": order_x_scales, "group_gate": group_gate, "quantize_gate": quantize_gate,
             "group_y": group_y, "quantize_y": quantize_y,
@@ -338,8 +346,9 @@ def tile_geglu_recompute_gate_descent_k3_kernel(
         nc.vector.memset(x_plane_raw[:].bitcast(I32), 0)
         nc.vector.memset(zero_in[:], 0.0)
         nc.scalar.activation(out=zero_bias[:], in_=zero_in[:], func=ACT.Silu)
-        nc.vector.memset(up_plane[:].bitcast(I32), 0)
-        nc.vector.memset(down_plane[:].bitcast(I32), 0)
+        for h in range(HALVES):
+            nc.vector.memset(up_plane[h][:].bitcast(I32), 0)
+            nc.vector.memset(down_plane[h][:].bitcast(I32), 0)
         nc.gpsimd.dma_start(out=rate_raw[:], in_=rate.rearrange("(g p t) o -> p g (t o)", p=P, t=PACK))
         for step in LOADS:
             run(step)

from contextlib import ExitStack

import concourse.mybir as mybir

T, D, F = 1024, 1024, 1536
C = 1.702
FLOPS = 3 * 2 * T * D * F

F32 = mybir.dt.float32
BF16 = mybir.dt.bfloat16
I32 = mybir.dt.int32
U8 = mybir.dt.uint8
FP8X4 = mybir.dt.float8_e4m3fn_x4
FP4X4 = mybir.dt.float4_e2m1fn_x4
ALU = mybir.AluOpType
ACT = mybir.ActivationFunctionType

P = 128
PACK = 4
SPAN = P * PACK
PASSES = D // SPAN
TOKEN_GROUPS = T // SPAN
QUADRANT = 32
ROWS = 4
BANK = 512
FP4_NARROW = 128
UP_ROW = 4

WIDTHS = [256, 512, 512, 256]
STARTS = [sum(WIDTHS[:c]) for c in range(len(WIDTHS))]
CHUNKS = len(WIDTHS)
GROUPS = CHUNKS * TOKEN_GROUPS
HALVES = 2
HALF_F = F // HALVES
UNITS = [
    (c, tg, t0)
    for c in range(CHUNKS)
    for tg in range(TOKEN_GROUPS)
    for t0 in range(0, PACK, BANK // WIDTHS[c])
]

PSUM_BUFS = {"a": 2, "u": 3, "e": 3}
PART_BUFS = {"silu": 5, "tanh": 4, "left": 4, "right": 5}

LOADS = [
    ("gate", 0, 0), ("x_scales",), ("gate", 0, 1), ("x_pass", 0), ("x_pass", 1), ("gate", 1, 0), ("x_second",),
    ("up_scales", 0), ("up", 0), ("gate", 1, 1), ("down_scales", 0), ("down", 0), ("gate", 3, 0), ("up", 1),
    ("down", 1), ("gate", 2, 0), ("gate", 2, 1), ("gate", 3, 1), ("up_scales", 1), ("down_scales", 1),
    ("up", 2), ("down", 2), ("up", 3), ("down", 3),
]

HEAD = [
    ("group_gate", "scalar", 0, 0, 0, 128), ("group_gate", "vector", 0, 0, 128, 256), ("order_x_scales", 0),
    ("group_gate", "scalar", 0, 1, 0, 128), ("group_gate", "scalar", 0, 1, 128, 256), ("order_x_pass", 0),
    ("quantize_gate", 0, 0), ("order_x_pass", 1), ("quantize_gate", 0, 1), ("order_x_scales", 1),
    ("group_gate", "vector", 1, 0, 0, 256), ("group_gate", "vector", 1, 0, 256, 512), ("order_x_second",),
    ("quantize_gate", 1, 0),
]

FIRST_PRODUCTS = {
    0: [("a", 0), ("a", 1), ("u", 0), ("u", 1)],
    1: [("u", 2), ("a", 2), ("e", 1), ("e", 0)],
    2: [],
    3: [("a", 3), ("u", 3), ("e", 3), ("e", 2)],
}

SCALAR_AFTER_ACTIVATIONS = {
    1: ("group_gate", "scalar", 1, 1, 0, 256), 2: ("group_gate", "scalar", 3, 0, 0, 256),
    3: ("group_gate", "scalar", 2, 0, 0, 256), 5: ("group_y", "scalar", 0, 0, 256),
    7: ("group_gate", "scalar", 2, 1, 0, 256), 9: ("group_gate", "scalar", 3, 1, 0, 256),
    11: ("group_y", "scalar", 1, 0, 256), 13: ("group_y", "scalar", 2, 0, 256),
    15: ("group_y", "scalar", 2, 256, 512), 17: ("group_y", "scalar", 3, 0, 256),
    19: ("group_y", "scalar", 3, 256, 512), 21: ("group_y", "scalar", 4, 0, 256),
    23: ("group_y", "scalar", 4, 256, 512),
}
VECTOR_AFTER_PSUM_READS = {0: ("group_gate", "vector", 1, 1, 256, 512), 13: ("quantize_y", 0)}
VECTOR_AFTER_FINISH = {
    1: ("quantize_gate", 1, 1), 3: ("group_gate", "vector", 2, 0, 256, 512),
    5: ("group_gate", "vector", 2, 1, 256, 512), 7: ("quantize_gate", 2, 0), 9: ("quantize_gate", 2, 1),
    11: ("quantize_gate", 3, 0), 13: ("quantize_gate", 3, 1), 15: ("quantize_y", 1), 17: ("quantize_y", 2),
    19: ("quantize_y", 3), 21: ("group_y", "vector", 5, 256, 512),
}
TAIL = [
    ("group_y", "scalar", 5, 0, 256), ("group_y", "scalar", 6, 0, 256), ("quantize_y", 4), ("quantize_y", 5),
    ("group_y", "scalar", 7, 0, 256), ("quantize_y", 6), ("quantize_y", 7),
]


def tile_geglu_recompute_gate_descent_k3_kernel(
    tc, x_words, x_scales, w_gate, up_words, up_scales, down_words, down_scales, rate, out_0, out_1, out_2
):
    nc = tc.nc
    with ExitStack() as ctx:
        keep = ctx.enter_context(tc.tile_pool(name="keep", bufs=1))
        work = ctx.enter_context(tc.tile_pool(name="work", bufs=1))
        psum = ctx.enter_context(tc.psum_pool(name="psum", bufs=1))
        ctx.enter_context(tc.manual_schedule())

        def kept(name, shape, dtype):
            return keep.tile(shape, dtype, name=name, align_bytes=64)

        x_raw = [kept("x_raw%d" % tg, [P, PASSES, SPAN], I32) for tg in range(TOKEN_GROUPS)]
        x_codes = [kept("x_codes%d" % tg, [P, PASSES, PACK, P], I32) for tg in range(TOKEN_GROUPS)]
        x_plane_raw = kept("x_plane_raw", [P, PASSES, T], U8)
        x_plane = [kept("x_plane%d" % tg, [P, PASSES, PACK, P], U8) for tg in range(TOKEN_GROUPS)]
        gate_raw = [kept("gate_raw%d" % c, [P, PASSES, PACK, w], BF16) for c, w in enumerate(WIDTHS)]
        gate_grouped = [kept("gate_grouped%d" % c, [P, PASSES, w, PACK], BF16) for c, w in enumerate(WIDTHS)]
        gate_codes = [kept("gate_codes%d" % c, [P, PASSES, w], I32) for c, w in enumerate(WIDTHS)]
        gate_plane = [kept("gate_plane%d" % c, [P, PASSES, w], U8) for c, w in enumerate(WIDTHS)]
        up_codes = [kept("up_codes%d" % c, [P, PASSES, w], I32) for c, w in enumerate(WIDTHS)]
        up_plane = [kept("up_plane%d" % h, [P, PASSES, HALF_F], U8) for h in range(HALVES)]
        down_codes = [kept("down_codes%d" % c, [P, PASSES, 2 * w], U8) for c, w in enumerate(WIDTHS)]
        down_plane = [kept("down_plane%d" % h, [P, PASSES, HALF_F], U8) for h in range(HALVES)]
        rate_raw = kept("rate_raw", [P, TOKEN_GROUPS, PACK], BF16)
        minus_half_rate = kept("minus_half_rate", [P, TOKEN_GROUPS, PACK], F32)
        half_rate = kept("half_rate", [P, TOKEN_GROUPS, PACK], F32)
        zero_in = kept("zero_in", [P, 1], F32)
        zero_bias = kept("zero_bias", [P, 1], F32)
        y = [kept("y%d" % j, [P, PACK, WIDTHS[j // TOKEN_GROUPS]], F32) for j in range(GROUPS)]
        y_grouped = [kept("y_grouped%d" % j, [P, WIDTHS[j // TOKEN_GROUPS], PACK], BF16) for j in range(GROUPS)]
        y_codes = [kept("y_codes%d" % c, [P, TOKEN_GROUPS, w], I32) for c, w in enumerate(WIDTHS)]
        y_plane = [kept("y_plane%d" % h, [P, TOKEN_GROUPS, HALF_F], U8) for h in range(HALVES)]

        x_src = x_words.rearrange("g p n t -> p g (n t)").bitcast(I32)
        up_src = up_words.rearrange("g p n t -> p g (n t)").bitcast(I32)
        down_src = down_words.rearrange("g p b -> p g b").bitcast(I32)
        codes_dst = out_1.rearrange("g p n t -> p g (n t)").bitcast(I32)
        y_dst = out_0.rearrange("(g p t) n -> p g t n", p=P, t=PACK)

        def chunk_cols(c):
            return slice(STARTS[c], STARTS[c] + WIDTHS[c])

        def half_words(h):
            return slice(h * HALF_F // 4, (h + 1) * HALF_F // 4)

        def scale_rows(scales, r):
            return scales.bitcast(I32)[:, r::ROWS, :].rearrange("g q n -> q g n")

        def load_scales(plane, rows_of, first_row):
            for r in range(ROWS):
                nc.sync.dma_start(out=plane.bitcast(I32)[first_row + r :: QUADRANT], in_=rows_of(r))

        def load_x_scales():
            load_scales(x_plane_raw[:], lambda r: scale_rows(x_scales, r), 0)

        def load_up_scales(h):
            load_scales(up_plane[h][:], lambda r: scale_rows(up_scales, r)[:, :, half_words(h)], UP_ROW)

        def load_down_scales(h):
            load_scales(down_plane[h][:], lambda r: scale_rows(down_scales, r)[:, :, half_words(h)], 0)

        def load_x_pass(g):
            nc.sync.dma_start(out=x_raw[0][:, g], in_=x_src[:, g, 0:SPAN])

        def load_x_second():
            nc.sync.dma_start(out=x_raw[1][:], in_=x_src[:, :, SPAN : 2 * SPAN])

        def load_gate(c, g):
            rows = w_gate[SPAN * g : SPAN * (g + 1), chunk_cols(c)]
            nc.sync.dma_start(out=gate_raw[c][:, g], in_=rows.rearrange("(p j) n -> p j n", j=PACK))

        def load_up(c):
            nc.sync.dma_start(out=up_codes[c][:], in_=up_src[:, :, chunk_cols(c)])

        def load_down(c):
            nc.sync.dma_start(
                out=down_codes[c][:].bitcast(I32),
                in_=down_src[:, :, STARTS[c] // 2 : (STARTS[c] + WIDTHS[c]) // 2],
            )

        def order_x_pass(g):
            nc.vector.tensor_copy(
                out=x_codes[0][:, g].rearrange("p t m -> p m t"),
                in_=x_raw[0][:, g].rearrange("p (m t) -> p m t", t=PACK),
            )

        def order_x_second():
            nc.vector.tensor_copy(
                out=x_codes[1][:].rearrange("p g t m -> p g m t"),
                in_=x_raw[1][:].rearrange("p g (m t) -> p g m t", t=PACK),
            )

        def order_x_scales(tg):
            nc.vector.tensor_copy(
                out=x_plane[tg][:],
                in_=x_plane_raw[:, :, SPAN * tg : SPAN * (tg + 1)].rearrange("p g (m t) -> p g t m", t=PACK),
            )

        def interleave(engine, dst, src, run):
            out = dst.rearrange("p (c i) t -> p c t i", i=run)
            in_ = src.rearrange("p t (c i) -> p c t i", i=run)
            if engine == "vector":
                nc.vector.tensor_copy(out=out, in_=in_)
            else:
                nc.scalar.copy(out=out, in_=in_)

        def group_gate(engine, c, g, lo, hi):
            interleave(engine, gate_grouped[c][:, g, lo:hi, :], gate_raw[c][:, g, :, lo:hi], 4)

        def quantize_gate(c, g):
            nc.vector.quantize_mx(
                out=gate_codes[c][:, g].bitcast(FP8X4),
                scales=gate_plane[c][:, g],
                in_=gate_grouped[c][:, g].rearrange("p n t -> p (n t)"),
            )

        def group_y(engine, j, lo, hi):
            interleave(engine, y_grouped[j][:, lo:hi, :], y[j][:, :, lo:hi], 2)

        def store_y_scales(h):
            for r in range(ROWS):
                queue = nc.scalar if h == HALVES - 1 and r % 2 == 1 else nc.sync
                queue.dma_start(
                    out=scale_rows(out_2, r)[:, :, half_words(h)], in_=y_plane[h][:].bitcast(I32)[r::QUADRANT]
                )

        def quantize_y(j):
            c, tg = divmod(j, TOKEN_GROUPS)
            h, lo = divmod(STARTS[c], HALF_F)
            nc.vector.quantize_mx(
                out=y_codes[c][:, tg].bitcast(FP8X4),
                scales=y_plane[h][:, tg, lo : lo + WIDTHS[c]],
                in_=y_grouped[j][:].rearrange("p n t -> p (n t)"),
            )
            if c < CHUNKS - 1:
                nc.sync.dma_start(out=codes_dst[:, tg, chunk_cols(c)], in_=y_codes[c][:, tg])
            elif tg == TOKEN_GROUPS - 1:
                nc.sync.dma_start(out=codes_dst[:, :, chunk_cols(c)], in_=y_codes[c][:])
            if tg == TOKEN_GROUPS - 1 and lo + WIDTHS[c] == HALF_F:
                store_y_scales(h)

        banks = {}
        parts = {}

        def slices_of(i):
            c, tg, t0 = UNITS[i]
            w = WIDTHS[c]
            return [(t0 + s, slice(w * s, w * (s + 1))) for s in range(BANK // w)]

        def moving_operand(name, c, g, lo, hi):
            if name == "a":
                return gate_codes[c][:, g, lo:hi].bitcast(FP8X4), gate_plane[c][:, g, lo:hi]
            h, start = divmod(STARTS[c], HALF_F)
            cols = slice(start + lo, start + hi)
            if name == "u":
                return up_codes[c][:, g, lo:hi].bitcast(FP8X4), up_plane[h][UP_ROW:, g, cols]
            return down_codes[c][:, g, 2 * lo : 2 * hi].bitcast(FP4X4), down_plane[h][:, g, cols]

        def product(name, i):
            c, tg, t0 = UNITS[i]
            n = FP4_NARROW if name == "e" and WIDTHS[c] < BANK else WIDTHS[c]
            acc = psum.tile([P, BANK], F32, name=name, tag=name, bufs=PSUM_BUFS[name])
            for t, cols in slices_of(i):
                for lo in range(0, WIDTHS[c], n):
                    for g in range(PASSES):
                        codes, plane = moving_operand(name, c, g, lo, lo + n)
                        nc.tensor.matmul_mx(
                            out=acc[:, cols.start + lo : cols.start + lo + n],
                            lhsT=x_codes[tg][:, g, t].bitcast(FP8X4),
                            lhsT_scale=x_plane[tg][:, g, t],
                            rhs=codes,
                            rhs_scale=plane,
                            start=(g == 0),
                            stop=(g == PASSES - 1),
                        )
            banks[name, i] = acc

        def part(name, i):
            parts[name, i] = work.tile([P, BANK], F32, name=name, tag=name, bufs=PART_BUFS[name])
            return parts[name, i]

        def activations(i):
            a = banks["a", i]
            nc.scalar.activation(out=part("silu", i)[:], in_=a[:], func=ACT.Silu, bias=zero_bias[:], scale=-C)
            nc.scalar.activation(out=part("tanh", i)[:], in_=a[:], func=ACT.Tanh, bias=zero_bias[:], scale=C / 2)

        def left_factor(i):
            nc.vector.scalar_tensor_tensor(
                out=part("left", i)[:], in0=parts["tanh", i][:], scalar=1.0, in1=banks["u", i][:],
                op0=ALU.add, op1=ALU.mult,
            )

        def right_factor(i):
            nc.vector.scalar_tensor_tensor(
                out=part("right", i)[:], in0=parts["silu", i][:], scalar=1.0, in1=banks["e", i][:],
                op0=ALU.subtract, op1=ALU.mult,
            )

        def left_times_e(i):
            nc.vector.tensor_tensor(
                out=part("right", i)[:], in0=parts["left", i][:], in1=banks["e", i][:], op=ALU.mult
            )

        def store_y(i):
            c, tg, t0 = UNITS[i]
            rows = slice(t0, t0 + BANK // WIDTHS[c])
            nc.sync.dma_start(out=y_dst[:, tg, rows, chunk_cols(c)], in_=y[TOKEN_GROUPS * c + tg][:, rows])

        def finish_on_vector(i):
            c, tg, t0 = UNITS[i]
            for t, cols in slices_of(i):
                nc.vector.scalar_tensor_tensor(
                    out=y[TOKEN_GROUPS * c + tg][:, t], in0=parts["left", i][:, cols],
                    scalar=minus_half_rate[:, tg, t : t + 1], in1=parts["right", i][:, cols],
                    op0=ALU.mult, op1=ALU.mult,
                )
            store_y(i)

        def finish_on_gpsimd(i):
            c, tg, t0 = UNITS[i]
            rated = parts["right", i + 1]
            for t, cols in slices_of(i):
                nc.gpsimd.tensor_scalar(
                    out=rated[:, cols], in0=parts["silu", i][:, cols],
                    scalar1=minus_half_rate[:, tg, t : t + 1], scalar2=half_rate[:, tg, t : t + 1],
                    op0=ALU.mult, op1=ALU.add,
                )
            rows = slice(t0, t0 + BANK // WIDTHS[c])
            nc.gpsimd.tensor_tensor(
                out=y[TOKEN_GROUPS * c + tg][:, rows].rearrange("p t n -> p (t n)"),
                in0=parts["right", i][:], in1=rated[:], op=ALU.mult,
            )
            store_y(i)

        steps = {
            "x_scales": load_x_scales, "up_scales": load_up_scales, "down_scales": load_down_scales,
            "x_pass": load_x_pass, "x_second": load_x_second, "gate": load_gate,
            "up": load_up, "down": load_down, "order_x_pass": order_x_pass, "order_x_second": order_x_second,
            "order_x_scales": order_x_scales, "group_gate": group_gate, "quantize_gate": quantize_gate,
            "group_y": group_y, "quantize_y": quantize_y,
        }

        def run(step):
            steps[step[0]](*step[1:])

        def run_listed(table, i):
            if i in table:
                run(table[i])

        def products_and_activations(i):
            for name, unit in FIRST_PRODUCTS.get(i, [("u", i), ("a", i), ("e", i)]):
                product(name, unit)
            activations(i)
            run_listed(SCALAR_AFTER_ACTIVATIONS, i)

        nc.vector.memset(x_plane_raw[:].bitcast(I32), 0)
        nc.vector.memset(zero_in[:], 0.0)
        nc.scalar.activation(out=zero_bias[:], in_=zero_in[:], func=ACT.Silu)
        for h in range(HALVES):
            nc.vector.memset(up_plane[h][:].bitcast(I32), 0)
            nc.vector.memset(down_plane[h][:].bitcast(I32), 0)
        nc.gpsimd.dma_start(out=rate_raw[:], in_=rate.rearrange("(g p t) o -> p g (t o)", p=P, t=PACK))
        for step in LOADS:
            run(step)
        for scaled, by in ((minus_half_rate, -0.5), (half_rate, 0.5)):
            nc.gpsimd.tensor_scalar(
                out=scaled[:], in0=rate_raw[:], scalar1=by, scalar2=0.0, op0=ALU.mult, op1=ALU.add
            )
        for step in HEAD:
            run(step)

        last_pair = len(UNITS) - 2
        for first in range(0, len(UNITS), 2):
            second = first + 1
            products_and_activations(first)
            if first > 0:
                finish_on_gpsimd(first - 2)
            left_factor(first)
            if first == last_pair:
                right_factor(first)
            run_listed(VECTOR_AFTER_PSUM_READS, first)
            products_and_activations(second)
            left_factor(second)
            right_factor(second)
            if first == last_pair:
                finish_on_vector(first)
            else:
                left_times_e(first)
            run_listed(VECTOR_AFTER_PSUM_READS, second)
            finish_on_vector(second)
            run_listed(VECTOR_AFTER_FINISH, second)
        for step in TAIL:
            run(step)
